import numpy as np
import ml_dtypes


def mxq(x, axis, fmt="e4m3"):
    dtype, down = {"e4m3": (ml_dtypes.float8_e4m3fn, 7), "e5m2": (ml_dtypes.float8_e5m2, 14)}[fmt]
    v = np.moveaxis(np.asarray(x, np.float32).astype(ml_dtypes.bfloat16).astype(np.float64), axis, -1)
    blocks = v.reshape(v.shape[:-1] + (-1, 32))
    amax = np.abs(blocks).max(-1, keepdims=True)
    byte = np.maximum(np.where(amax > 0, np.frexp(amax)[1] - 1 + 127, 0) - down, 1)
    scale = np.exp2(byte - 127.0)
    codes = (blocks / scale).astype(np.float32).astype(dtype).astype(np.float64)
    return np.moveaxis((codes * scale).reshape(v.shape), -1, axis)


WIDE = False


def mx_kscale(k):
    if not WIDE:
        return np.ones(k)
    levels = np.array([10, -10, 5, -5, 0])
    if k % 512:
        return np.exp2(np.random.permutation(np.resize(levels, k // 32))).repeat(32)
    a = np.empty((k // 512, 16))
    for p in range(k // 512):
        a[p, :8] = np.random.permutation(np.resize(levels, 8))
        for g in range(8):
            far = levels[np.abs(levels - a[p, g]) >= 10]
            a[p, g + 8] = far[np.random.randint(len(far))]
    return np.exp2(a.ravel()).repeat(32)


BF16 = ml_dtypes.bfloat16


def bf(x):
    return np.asarray(x, np.float32).astype(BF16)


def f64(x):
    return np.asarray(x).astype(np.float64)


E2M1 = np.array([0.0, 0.5, 1.0, 1.5, 2.0, 3.0, 4.0, 6.0, -0.0, -0.5, -1.0, -1.5, -2.0, -3.0, -4.0, -6.0])


def pack_weight(w, fmt):
    k, n = w.shape
    w = f64(bf(w)).reshape(k // 32, 32, n)
    amax = np.abs(w).max(1)
    if fmt == "e4m3":
        byte = np.frexp(amax)[1] - 1 + 127 - 7
    else:
        mant, ex = np.frexp(amax / 6.0)
        byte = np.where(mant > 0.5, ex, ex - 1) + 127
    byte = np.clip(np.where(amax > 0, byte, 1), 1, 254)
    scaled = (w * np.exp2(127.0 - byte)[:, None, :]).reshape(k, n).astype(np.float32)
    by_word = np.ascontiguousarray(scaled.reshape(k // 512, 128, 4, n).transpose(0, 1, 3, 2))
    if fmt == "e4m3":
        words = by_word.astype(ml_dtypes.float8_e4m3fn).view(np.uint8)
    else:
        c = by_word.astype(ml_dtypes.float4_e2m1fn).view(np.uint8) & 0xF
        words = c[..., 0::2] | (c[..., 1::2] << 4)
    return np.ascontiguousarray(words), np.ascontiguousarray(byte.astype(np.uint8).reshape(k // 512, 16, n))


def unpack_weight(words, scales, fmt):
    g, p, n, _ = words.shape
    if fmt == "e4m3":
        vals = np.ascontiguousarray(words).view(ml_dtypes.float8_e4m3fn).astype(np.float64)
    else:
        nib = np.empty((g, p, n, 4), np.uint8)
        nib[..., 0::2] = words & 0xF
        nib[..., 1::2] = words >> 4
        vals = E2M1[nib]
    vals = vals * np.repeat(np.exp2(scales.astype(np.float64) - 127.0), 8, axis=1)[..., None]
    return vals.transpose(0, 1, 3, 2).reshape(g * 512, n)
def pack4(w):
    words, scales = pack_weight(w, "e2m1")
    return words.reshape(words.shape[0], 128, -1), scales


def unpack4(words, scales):
    return unpack_weight(words.reshape(words.shape[0], 128, -1, 2), scales, "e2m1")


K, N = 1024, 1536


def setup_inputs():
    s = mx_kscale(K)
    a = np.random.standard_normal((K, K)) / np.sqrt(K)
    gram = np.eye(K) + (a + a.T) / np.sqrt(2.0)
    damp = 0.3 * (1 + 0.1 * np.random.standard_normal(K))
    e4 = np.random.standard_normal((K, N)) / s[:, None]
    e8 = 0.7 * np.random.standard_normal((K, N)) / s[:, None]
    e16 = 0.5 * np.random.standard_normal((K, N)) / s[:, None]
    e4_words, e4_scales = pack4(e4)
    e8_words, e8_scales = pack_weight(e8, "e4m3")
    return {"gram": bf(gram * s),
            "damp": bf(damp * s),
            "e4_words": e4_words, "e4_scales": e4_scales,
            "e8_words": e8_words, "e8_scales": e8_scales,
            "e16": bf(e16),
            "step4": bf(1 + 0.1 * np.random.standard_normal(N)),
            "step8": bf(1 + 0.1 * np.random.standard_normal(N))}


def reference(gram, damp, e4_words, e4_scales, e8_words, e8_scales, e16, step4, step8):
    h = mxq(f64(gram) + np.eye(K) * f64(damp), 1, "e4m3")
    r4 = h @ unpack4(e4_words, e4_scales)
    r8 = h @ unpack_weight(e8_words, e8_scales, "e4m3")
    r16 = h @ mxq(f64(e16), 0, "e4m3")
    return r4 * f64(step4) + r8 * f64(step8) + r16

@@ -1,0 +1,313 @@
+from contextlib import ExitStack
+
+import concourse.mybir as mybir
+from concourse.masks import make_identity
+
+K, N = 1024, 1536
+FLOPS = 3 * 2 * K * K * N
+
+F32 = mybir.dt.float32
+BF16 = mybir.dt.bfloat16
+I32 = mybir.dt.int32
+U32 = mybir.dt.uint32
+U8 = mybir.dt.uint8
+FP8X4 = mybir.dt.float8_e4m3fn_x4
+FP4X4 = mybir.dt.float4_e2m1fn_x4
+MULT = mybir.AluOpType.mult
+ADD = mybir.AluOpType.add
+
+P = 128
+PASSES = 2
+NT = 512
+COLS = N // NT
+ROWS = K // P
+UNITS = ROWS * COLS
+BANKS = 8
+E8_PLANE = 4
+TAIL = 3
+
+
+def tile_damped_gram_error_s10_kernel(
+    tc, gram, damp, e4_words, e4_scales, e8_words, e8_scales, e16, step4, step8, out
+):
+    nc = tc.nc
+    with ExitStack() as ctx:
+        keep = ctx.enter_context(tc.tile_pool(name="keep", bufs=1))
+        sums = ctx.enter_context(tc.tile_pool(name="sums", bufs=1))
+        psum = ctx.enter_context(tc.psum_pool(name="psum", bufs=1))
+        ctx.enter_context(tc.manual_schedule())
+
+        turn = [0]
+
+        def bank():
+            b = turn[0] % BANKS
+            turn[0] = turn[0] + 1
+            return psum.tile([P, NT], F32, name="bank%d" % b, tag="bank%d" % b)
+
+        def kept(name, shape, dtype):
+            return keep.tile(shape, dtype, name=name, tag=name, align_bytes=64)
+
+        ident = kept("ident", [P, P], F32)
+        make_identity(nc, ident[:])
+        e8_plane = kept("e8_plane", [P, PASSES * N], U8)
+        e4_plane = kept("e4_plane", [P, PASSES * N], U8)
+        nc.vector.memset(e8_plane[:].bitcast(I32), 0)
+        nc.vector.memset(e4_plane[:].bitcast(I32), 0)
+
+        gram_rows = gram.rearrange("(c p e) k -> c p e k", p=P, e=2)
+        out_rows = out.rearrange("(c p e) n -> c e p n", p=P, e=2)
+        damp_sb = kept("damp_sb", [P, ROWS // 2, 2], BF16)
+        nc.sync.dma_start(out=damp_sb[:], in_=damp.rearrange("(c p e) -> p c e", p=P, e=2))
+
+        g_tile = {}
+
+        def load_gram_row(i):
+            t = kept("gram%d" % i, [P, K], BF16)
+            nc.sync.dma_start(out=t[:], in_=gram_rows[i // 2, :, i % 2, :])
+            g_tile[i] = (t, 0)
+
+        def load_gram_pair(c):
+            t = kept("gram%d" % (2 * c), [P, 2 * K], BF16)
+            nc.sync.dma_start(out=t[:], in_=gram_rows[c].rearrange("p e k -> p (e k)"))
+            g_tile[2 * c] = (t, 0)
+            g_tile[2 * c + 1] = (t, K)
+
+        e8_tile, e4_tile, e16_tile = {}, {}, {}
+
+        def load_words(j0, j1):
+            w = (j1 - j0) * NT
+            t8 = kept("e8_codes%d" % j0, [P, PASSES, w], U32)
+            src8 = e8_words.rearrange("g p n t -> p g (n t)")[:, :, 4 * NT * j0 : 4 * NT * j1]
+            nc.sync.dma_start(out=t8[:].bitcast(I32), in_=src8.bitcast(I32))
+            for j in range(j0, j1):
+                e8_tile[j] = (t8, (j - j0) * NT)
+
+        def load_nibbles(j0, j1):
+            w = (j1 - j0) * NT
+            t4 = kept("e4_codes%d" % j0, [P, PASSES, 2 * w], U8)
+            src4 = e4_words.rearrange("g p b -> p g b")[:, :, 2 * NT * j0 : 2 * NT * j1]
+            nc.sync.dma_start(out=t4[:].bitcast(I32), in_=src4.bitcast(I32))
+            for j in range(j0, j1):
+                e4_tile[j] = (t4, (j - j0) * NT)
+
+        def load_plane(plane, scales, first):
+            rows = scales.bitcast(I32).rearrange("g (q r) n -> r q g n", r=4)
+            for r in range(4):
+                dst = plane[:].bitcast(I32)[first + r : P : 32, :]
+                nc.sync.dma_start(out=dst.rearrange("q (g n) -> q g n", g=PASSES), in_=rows[r])
+
+        def load_e16(g, j0, j1):
+            t = kept("e16_raw%d_%d" % (g, j0), [P, 4, (j1 - j0) * NT], BF16)
+            src = e16.rearrange("(g p t) n -> g p t n", p=P, t=4)[g, :, :, NT * j0 : NT * j1]
+            nc.sync.dma_start(out=t[:], in_=src)
+            for j in range(j0, j1):
+                e16_tile[g, j] = (t, (j - j0) * NT)
+
+        step_cols = [kept("step8_cols", [P, COLS, 4], BF16), kept("step4_cols", [P, COLS, 4], BF16)]
+
+        load_gram_row(0)
+        load_gram_row(1)
+        load_words(0, 1)
+        load_plane(e8_plane, e8_scales, E8_PLANE)
+        nc.sync.dma_start(out=step_cols[0][:], in_=step8.rearrange("(j p c) -> p j c", p=P, c=4))
+        nc.sync.dma_start(out=step_cols[1][:], in_=step4.rearrange("(j p c) -> p j c", p=P, c=4))
+        load_nibbles(0, 1)
+        load_plane(e4_plane, e4_scales, 0)
+        for c in range(1, ROWS // 2):
+            load_gram_pair(c)
+        for g in range(PASSES):
+            load_e16(g, 0, 1)
+        load_words(1, COLS)
+        load_nibbles(1, COLS)
+        for g in range(PASSES):
+            load_e16(g, 1, COLS)
+
+        h_grouped, h_codes = {}, {}
+
+        def add_damp(i):
+            t, base = g_tile[i]
+            c, e = divmod(i, 2)
+            first = base + 2 * P * c + e
+            diag = t[:, first : base + 2 * P * (c + 1) : 2]
+            nc.vector.scalar_tensor_tensor(
+                out=diag, in0=ident[:], scalar=damp_sb[:, c, e : e + 1], in1=diag, op0=MULT, op1=ADD
+            )
+
+        def turn_h(i, group):
+            t, base = g_tile[i]
+            words = t[:].bitcast(F32)
+            xt = bank()
+            for g in reversed(range(PASSES)):
+                for u in range(2):
+                    lo = base // 2 + 2 * P * g
+                    slot = 2 * g + u
+                    nc.tensor.transpose(xt[:, slot * P : (slot + 1) * P], words[:, lo + u : lo + 2 * P : 2], ident[:])
+            if group[0] not in h_grouped:
+                h_grouped[group[0]] = kept("h_grouped%d" % group[0], [P, len(group) * K], BF16)
+            dst = h_grouped[group[0]][:].bitcast(F32)[:, (i - group[0]) * NT : (i - group[0] + 1) * NT]
+            nc.scalar.copy(
+                out=dst.rearrange("p (g m u) -> p g m u", g=PASSES, u=2),
+                in_=xt[:].rearrange("p (g u m) -> p g m u", g=PASSES, u=2),
+            )
+
+        def quantise_h(group):
+            w = len(group) * PASSES * P
+            codes = kept("h_codes%d" % group[0], [P, w], U32)
+            plane = kept("h_plane%d" % group[0], [P, w], U8)
+            nc.vector.quantize_mx(out=codes[:].bitcast(FP8X4), scales=plane[:], in_=h_grouped[group[0]][:])
+            for i in group:
+                h_codes[i] = (codes, plane, (i - group[0]) * PASSES * P)
+
+        steps = {}
+
+        def spread_steps(j):
+            xt = bank()
+            for v in range(2):
+                cols = step_cols[v][:].rearrange("p j c -> p (j c)").bitcast(F32)
+                for c in range(2):
+                    w = 2 * j + c
+                    slot = 2 * v + c
+                    nc.tensor.transpose(
+                        xt[:, slot * P : (slot + 1) * P], cols[:, w : w + 1].to_broadcast([P, P]), ident[:]
+                    )
+            steps[j] = kept("steps%d" % j, [P, 2 * NT], BF16)
+            nc.scalar.copy(
+                out=steps[j][:].bitcast(F32).rearrange("p (v n c) -> p v n c", v=2, c=2),
+                in_=xt[:].rearrange("p (v c n) -> p v n c", v=2, c=2),
+            )
+
+        e16_grouped, e16_codes = {}, {}
+
+        def group_e16(g, j, half):
+            raw, base = e16_tile[g, j]
+            if half == 0:
+                e16_grouped[g, j] = kept("e16_grouped%d_%d" % (g, j), [P, 4 * NT], BF16)
+            w = NT // 2
+            dst = e16_grouped[g, j][:, 4 * w * half : 4 * w * (half + 1)]
+            src = raw[:, :, base + w * half : base + w * (half + 1)]
+            nc.scalar.copy(
+                out=dst.rearrange("p (c i t) -> p c t i", i=4, t=4),
+                in_=src.rearrange("p t (c i) -> p c t i", i=4),
+            )
+
+        def quantise_e16(g, j):
+            codes = kept("e16_codes%d_%d" % (g, j), [P, NT], U32)
+            plane = kept("e16_plane%d_%d" % (g, j), [P, NT], U8)
+            nc.vector.quantize_mx(out=codes[:].bitcast(FP8X4), scales=plane[:], in_=e16_grouped[g, j][:])
+            e16_codes[g, j] = (codes, plane)
+
+        def product(i, moving):
+            codes, plane, base = h_codes[i]
+            acc = bank()
+            for g in range(PASSES):
+                cols = slice(base + g * P, base + (g + 1) * P)
+                rhs, rhs_scale = moving(g)
+                nc.tensor.matmul_mx(
+                    out=acc[:],
+                    lhsT=codes[:, cols].bitcast(FP8X4),
+                    lhsT_scale=plane[:, cols],
+                    rhs=rhs,
+                    rhs_scale=rhs_scale,
+                    start=(g == 0),
+                    stop=(g == PASSES - 1),
+                )
+            return acc
+
+        scaled = {}
+
+        def stepped_products(unit, between=None):
+            j, i = divmod(unit, ROWS)
+            t8, b8 = e8_tile[j]
+            t4, b4 = e4_tile[j]
+            r8 = product(
+                i,
+                lambda g: (
+                    t8[:, g, b8 : b8 + NT].bitcast(FP8X4),
+                    e8_plane[E8_PLANE:P, g * N + j * NT : g * N + (j + 1) * NT],
+                ),
+            )
+            r4 = product(
+                i,
+                lambda g: (
+                    t4[:, g, 2 * b4 : 2 * (b4 + NT)].bitcast(FP4X4),
+                    e4_plane[:, g * N + j * NT : g * N + (j + 1) * NT],
+                ),
+            )
+            part8 = sums.tile([P, NT], F32, name="part8", tag="part8", bufs=4)
+            total = sums.tile([P, NT], F32, name="total", tag="total", bufs=14)
+            nc.vector.tensor_tensor(out=part8[:], in0=r8[:], in1=steps[j][:, 0:NT], op=MULT)
+            if between is not None:
+                between()
+            nc.vector.tensor_tensor(out=total[:], in0=r4[:], in1=steps[j][:, NT : 2 * NT], op=MULT)
+            nc.gpsimd.tensor_tensor(out=total[:], in0=total[:], in1=part8[:], op=ADD)
+            scaled[unit] = total
+
+        def plain_product(unit):
+            j, i = divmod(unit, ROWS)
+            r16 = product(i, lambda g: (e16_codes[g, j][0][:].bitcast(FP8X4), e16_codes[g, j][1][:]))
+            total = scaled[unit]
+            if unit % 3 == 1 and unit < UNITS - TAIL:
+                part16 = sums.tile([P, NT], F32, name="part16", tag="part16", bufs=3)
+                nc.scalar.copy(out=part16[:], in_=r16[:])
+                nc.gpsimd.tensor_tensor(out=total[:], in0=total[:], in1=part16[:], op=ADD)
+            else:
+                nc.vector.tensor_tensor(out=total[:], in0=r16[:], in1=total[:], op=ADD)
+            nc.sync.dma_start(out=out_rows[i // 2, i % 2, :, j * NT : (j + 1) * NT], in_=total[:])
+
+        add_damp(0)
+        add_damp(1)
+        turn_h(0, [0])
+        turn_h(1, [1])
+        quantise_h([0])
+        spread_steps(0)
+        quantise_h([1])
+        add_damp(2)
+        add_damp(3)
+        stepped_products(0, lambda: (add_damp(4), add_damp(5)))
+        turn_h(2, [2, 3])
+        turn_h(3, [2, 3])
+        turn_h(4, [4, 5])
+        turn_h(5, [4, 5])
+        add_damp(6)
+        add_damp(7)
+        quantise_h([2, 3])
+        stepped_products(1)
+        quantise_h([4, 5])
+        turn_h(6, [6, 7])
+        turn_h(7, [6, 7])
+        spread_steps(1)
+        spread_steps(2)
+        stepped_products(2)
+        group_e16(0, 0, 0)
+        group_e16(0, 0, 1)
+        stepped_products(3)
+        quantise_h([6, 7])
+        group_e16(1, 0, 0)
+        group_e16(1, 0, 1)
+        stepped_products(4)
+        stepped_products(5)
+        quantise_e16(0, 0)
+        stepped_products(6)
+        quantise_e16(1, 0)
+        stepped_products(7)
+
+        later = [(g, j) for j in range(1, COLS) for g in range(PASSES)]
+        done = 0
+        rest = UNITS - ROWS
+        for step in range(rest):
+            if step // 2 < len(later):
+                g, j = later[step // 2]
+                group_e16(g, j, step % 2)
+            want = (step + 1) * (UNITS - TAIL) // rest
+            while done < want - 1:
+                plain_product(done)
+                done = done + 1
+            stepped_products(ROWS + step)
+            if step % 2 == 0 and 0 < step <= 2 * len(later):
+                quantise_e16(*later[step // 2 - 1])
+            while done < want:
+                plain_product(done)
+                done = done + 1
+        while done < UNITS:
+            plain_product(done)
+            done = done + 1

@@ -15,16 +15,23 @@ FP8X4 = mybir.dt.float8_e4m3fn_x4
 FP4X4 = mybir.dt.float4_e2m1fn_x4
 MULT = mybir.AluOpType.mult
 ADD = mybir.AluOpType.add
+COPY = mybir.ActivationFunctionType.Copy
 
 P = 128
 PASSES = 2
 NT = 512
 COLS = N // NT
 ROWS = K // P
-UNITS = ROWS * COLS
+HALF = ROWS // 2
 BANKS = 8
 E8_PLANE = 4
+TURNED_COL = 0
+TOTALS = 16
 TAIL = 3
+BACK = 11
+QUANT = {6: 1, 10: 2}
+SHED = ()
+GROUP = {2 + n: [(1 + n // 4, n % 4)] for n in range(8)}
 
 
 def tile_damped_gram_error_s10_kernel(
@@ -37,29 +44,34 @@ def tile_damped_gram_error_s10_kernel(
         psum = ctx.enter_context(tc.psum_pool(name="psum", bufs=1))
         ctx.enter_context(tc.manual_schedule())
 
-        turn = [0]
+        free_banks = list(range(BANKS))
 
-        def bank():
-            b = turn[0] % BANKS
-            turn[0] = turn[0] + 1
-            return psum.tile([P, NT], F32, name="bank%d" % b, tag="bank%d" % b)
+        def take_bank():
+            b = free_banks.pop(0)
+            return b, psum.tile([P, NT], F32, name="bank%d" % b, tag="bank%d" % b)
 
         def kept(name, shape, dtype):
             return keep.tile(shape, dtype, name=name, tag=name, align_bytes=64)
 
         ident = kept("ident", [P, P], F32)
         make_identity(nc, ident[:])
-        e8_plane = kept("e8_plane", [P, PASSES * N], U8)
-        e4_plane = kept("e4_plane", [P, PASSES * N], U8)
-        nc.vector.memset(e8_plane[:].bitcast(I32), 0)
-        nc.vector.memset(e4_plane[:].bitcast(I32), 0)
+        planes = {}
+        for j0, j1 in ((0, 1), (1, COLS)):
+            for fmt in ("e8", "e4"):
+                t = kept("%s_plane%d" % (fmt, j0), [P, PASSES * (j1 - j0) * NT], U8)
+                nc.vector.memset(t[:].bitcast(I32), 0)
+                for j in range(j0, j1):
+                    planes[fmt, j] = (t, (j1 - j0) * NT, (j - j0) * NT)
+        step_rows = kept("step_rows", [P, P], BF16)
+        nc.vector.memset(step_rows[:], 0.0)
 
         gram_rows = gram.rearrange("(c p e) k -> c p e k", p=P, e=2)
         out_rows = out.rearrange("(c p e) n -> c e p n", p=P, e=2)
-        damp_sb = kept("damp_sb", [P, ROWS // 2, 2], BF16)
-        nc.sync.dma_start(out=damp_sb[:], in_=damp.rearrange("(c p e) -> p c e", p=P, e=2))
+        damp_sb = kept("damp_sb", [P, HALF, 2], BF16)
+        g_tile, e8_tile, e4_tile, e16_tile, step_words = {}, {}, {}, {}, {}
 
-        g_tile = {}
+        def load_damp():
+            nc.sync.dma_start(out=damp_sb[:], in_=damp.rearrange("(c p e) -> p c e", p=P, e=2))
 
         def load_gram_row(i):
             t = kept("gram%d" % i, [P, K], BF16)
@@ -72,26 +84,23 @@ def tile_damped_gram_error_s10_kernel(
             g_tile[2 * c] = (t, 0)
             g_tile[2 * c + 1] = (t, K)
 
-        e8_tile, e4_tile, e16_tile = {}, {}, {}
-
-        def load_words(j0, j1):
-            w = (j1 - j0) * NT
-            t8 = kept("e8_codes%d" % j0, [P, PASSES, w], U32)
-            src8 = e8_words.rearrange("g p n t -> p g (n t)")[:, :, 4 * NT * j0 : 4 * NT * j1]
-            nc.sync.dma_start(out=t8[:].bitcast(I32), in_=src8.bitcast(I32))
+        def load_e8(j0, j1):
+            t = kept("e8_codes%d" % j0, [P, PASSES, (j1 - j0) * NT], U32)
+            src = e8_words.rearrange("g p n t -> p g (n t)")[:, :, 4 * NT * j0 : 4 * NT * j1]
+            nc.sync.dma_start(out=t[:].bitcast(I32), in_=src.bitcast(I32))
             for j in range(j0, j1):
-                e8_tile[j] = (t8, (j - j0) * NT)
+                e8_tile[j] = (t, (j - j0) * NT)
 
-        def load_nibbles(j0, j1):
-            w = (j1 - j0) * NT
-            t4 = kept("e4_codes%d" % j0, [P, PASSES, 2 * w], U8)
-            src4 = e4_words.rearrange("g p b -> p g b")[:, :, 2 * NT * j0 : 2 * NT * j1]
-            nc.sync.dma_start(out=t4[:].bitcast(I32), in_=src4.bitcast(I32))
+        def load_e4(j0, j1):
+            t = kept("e4_codes%d" % j0, [P, PASSES, 2 * (j1 - j0) * NT], U8)
+            src = e4_words.rearrange("g p b -> p g b")[:, :, 2 * NT * j0 : 2 * NT * j1]
+            nc.sync.dma_start(out=t[:].bitcast(I32), in_=src.bitcast(I32))
             for j in range(j0, j1):
-                e4_tile[j] = (t4, (j - j0) * NT)
+                e4_tile[j] = (t, (j - j0) * NT)
 
-        def load_plane(plane, scales, first):
-            rows = scales.bitcast(I32).rearrange("g (q r) n -> r q g n", r=4)
+        def load_plane(fmt, scales, first, j0, j1):
+            plane = planes[fmt, j0][0]
+            rows = scales.bitcast(I32).rearrange("g (q r) n -> r q g n", r=4)[:, :, :, NT // 4 * j0 : NT // 4 * j1]
             for r in range(4):
                 dst = plane[:].bitcast(I32)[first + r : P : 32, :]
                 nc.sync.dma_start(out=dst.rearrange("q (g n) -> q g n", g=PASSES), in_=rows[r])
@@ -103,69 +112,68 @@ def tile_damped_gram_error_s10_kernel(
             for j in range(j0, j1):
                 e16_tile[g, j] = (t, (j - j0) * NT)
 
-        step_cols = [kept("step8_cols", [P, COLS, 4], BF16), kept("step4_cols", [P, COLS, 4], BF16)]
+        def load_steps(j0, j1):
+            for v, step in enumerate((step8, step4)):
+                t = kept("step_words%d_%d" % (v, j0), [P, j1 - j0, 4], BF16)
+                nc.sync.dma_start(out=t[:], in_=step.rearrange("(j p c) -> p j c", p=P, c=4)[:, j0:j1, :])
+                for j in range(j0, j1):
+                    step_words[v, j] = (t, j - j0)
 
-        load_gram_row(0)
-        load_gram_row(1)
-        load_words(0, 1)
-        load_plane(e8_plane, e8_scales, E8_PLANE)
-        nc.sync.dma_start(out=step_cols[0][:], in_=step8.rearrange("(j p c) -> p j c", p=P, c=4))
-        nc.sync.dma_start(out=step_cols[1][:], in_=step4.rearrange("(j p c) -> p j c", p=P, c=4))
-        load_nibbles(0, 1)
-        load_plane(e4_plane, e4_scales, 0)
-        for c in range(1, ROWS // 2):
-            load_gram_pair(c)
-        for g in range(PASSES):
-            load_e16(g, 0, 1)
-        load_words(1, COLS)
-        load_nibbles(1, COLS)
-        for g in range(PASSES):
-            load_e16(g, 1, COLS)
+        def load_step_rows():
+            for v, step in enumerate((step8, step4)):
+                rows = step.rearrange("(j b p) -> j b p", b=4, p=P)[TURNED_COL]
+                nc.sync.dma_start(out=step_rows[4 * v : 4 * v + 4, :], in_=rows)
 
-        h_grouped, h_codes = {}, {}
+        h_grouped = [kept("h_grouped%d" % h, [P, HALF * K], BF16) for h in range(2)]
+        h_codes = [kept("h_codes%d" % h, [P, PASSES * NT], U32) for h in range(2)]
+        h_plane = [kept("h_plane%d" % h, [P, PASSES * NT], U8) for h in range(2)]
 
         def add_damp(i):
             t, base = g_tile[i]
             c, e = divmod(i, 2)
-            first = base + 2 * P * c + e
-            diag = t[:, first : base + 2 * P * (c + 1) : 2]
+            diag = t[:, base + 2 * P * c + e : base + 2 * P * (c + 1) : 2]
             nc.vector.scalar_tensor_tensor(
                 out=diag, in0=ident[:], scalar=damp_sb[:, c, e : e + 1], in1=diag, op0=MULT, op1=ADD
             )
 
-        def turn_h(i, group):
+        def turn_h(i):
             t, base = g_tile[i]
             words = t[:].bitcast(F32)
-            xt = bank()
-            for g in reversed(range(PASSES)):
+            b, xt = take_bank()
+            for g in (1, 0):
                 for u in range(2):
                     lo = base // 2 + 2 * P * g
                     slot = 2 * g + u
                     nc.tensor.transpose(xt[:, slot * P : (slot + 1) * P], words[:, lo + u : lo + 2 * P : 2], ident[:])
-            if group[0] not in h_grouped:
-                h_grouped[group[0]] = kept("h_grouped%d" % group[0], [P, len(group) * K], BF16)
-            dst = h_grouped[group[0]][:].bitcast(F32)[:, (i - group[0]) * NT : (i - group[0] + 1) * NT]
-            nc.scalar.copy(
-                out=dst.rearrange("p (g m u) -> p g m u", g=PASSES, u=2),
-                in_=xt[:].rearrange("p (g u m) -> p g m u", g=PASSES, u=2),
+            dst = h_grouped[i // HALF][:].bitcast(F32).rearrange("p (i g m u) -> p i g m u", g=PASSES, i=HALF, u=2)
+            nc.scalar.copy(out=dst[:, i % HALF], in_=xt[:].rearrange("p (g u m) -> p g m u", g=PASSES, u=2))
+            free_banks.append(b)
+
+        def quantise_h(h, lo, hi, source):
+            nc.vector.quantize_mx(
+                out=h_codes[h][:, lo:hi].bitcast(FP8X4),
+                scales=h_plane[h][:, lo:hi],
+                in_=h_grouped[h][:, 4 * source : 4 * (source + hi - lo)],
             )
 
-        def quantise_h(group):
-            w = len(group) * PASSES * P
-            codes = kept("h_codes%d" % group[0], [P, w], U32)
-            plane = kept("h_plane%d" % group[0], [P, w], U8)
-            nc.vector.quantize_mx(out=codes[:].bitcast(FP8X4), scales=plane[:], in_=h_grouped[group[0]][:])
-            for i in group:
-                h_codes[i] = (codes, plane, (i - group[0]) * PASSES * P)
+        def quantise_h_tiles(i0, i1):
+            quantise_h(0, i0 * PASSES * P, i1 * PASSES * P, i0 * PASSES * P)
+
+        def quantise_h_by_pass(i):
+            for g in (1, 0):
+                lo = g * NT + (i - HALF) * P
+                quantise_h(1, lo, lo + P, ((i - HALF) * PASSES + g) * P)
 
         steps = {}
+        step_cols = kept("step_cols", [P, 8], F32)
 
         def spread_steps(j):
-            xt = bank()
+            b, xt = take_bank()
             for v in range(2):
-                cols = step_cols[v][:].rearrange("p j c -> p (j c)").bitcast(F32)
+                t, row = step_words[v, j]
+                cols = t[:].rearrange("p j c -> p (j c)").bitcast(F32)
                 for c in range(2):
-                    w = 2 * j + c
+                    w = 2 * row + c
                     slot = 2 * v + c
                     nc.tensor.transpose(
                         xt[:, slot * P : (slot + 1) * P], cols[:, w : w + 1].to_broadcast([P, P]), ident[:]
@@ -175,139 +183,241 @@ def tile_damped_gram_error_s10_kernel(
                 out=steps[j][:].bitcast(F32).rearrange("p (v n c) -> p v n c", v=2, c=2),
                 in_=xt[:].rearrange("p (v c n) -> p v n c", v=2, c=2),
             )
+            free_banks.append(b)
 
-        e16_grouped, e16_codes = {}, {}
+        step_rows32 = kept("step_rows32", [P, P], F32)
 
-        def group_e16(g, j, half):
+        def widen_step_rows():
+            nc.scalar.copy(out=step_rows32[:], in_=step_rows[:])
+
+        def turn_steps():
+            b, xt = take_bank()
+            nc.tensor.transpose(xt[:, 0:P], step_rows32[:], ident[:])
+            nc.scalar.copy(out=step_cols[:], in_=xt[:, 0:8])
+            free_banks.append(b)
+
+        e16_grouped = [kept("e16_grouped%d" % j, [P, PASSES * 4 * NT], BF16) for j in range(COLS)]
+        e16_codes = [kept("e16_codes%d" % j, [P, PASSES * NT], U32) for j in range(COLS)]
+        e16_plane = [kept("e16_plane%d" % j, [P, PASSES * NT], U8) for j in range(COLS)]
+
+        def group_e16(j, quarter, copy=nc.scalar.copy):
+            g, half = divmod(quarter, 2)
             raw, base = e16_tile[g, j]
-            if half == 0:
-                e16_grouped[g, j] = kept("e16_grouped%d_%d" % (g, j), [P, 4 * NT], BF16)
             w = NT // 2
-            dst = e16_grouped[g, j][:, 4 * w * half : 4 * w * (half + 1)]
+            dst = e16_grouped[j][:, 4 * w * quarter : 4 * w * (quarter + 1)]
             src = raw[:, :, base + w * half : base + w * (half + 1)]
-            nc.scalar.copy(
+            copy(
                 out=dst.rearrange("p (c i t) -> p c t i", i=4, t=4),
                 in_=src.rearrange("p t (c i) -> p c t i", i=4),
             )
 
-        def quantise_e16(g, j):
-            codes = kept("e16_codes%d_%d" % (g, j), [P, NT], U32)
-            plane = kept("e16_plane%d_%d" % (g, j), [P, NT], U8)
-            nc.vector.quantize_mx(out=codes[:].bitcast(FP8X4), scales=plane[:], in_=e16_grouped[g, j][:])
-            e16_codes[g, j] = (codes, plane)
+        def quantise_e16(j, g0=0, g1=PASSES):
+            nc.vector.quantize_mx(
+                out=e16_codes[j][:, g0 * NT : g1 * NT].bitcast(FP8X4),
+                scales=e16_plane[j][:, g0 * NT : g1 * NT],
+                in_=e16_grouped[j][:, 4 * g0 * NT : 4 * g1 * NT],
+            )
 
-        def product(i, moving):
-            codes, plane, base = h_codes[i]
-            acc = bank()
-            for g in range(PASSES):
-                cols = slice(base + g * P, base + (g + 1) * P)
-                rhs, rhs_scale = moving(g)
+        def e_operand(fmt, g, j, lo, hi):
+            if fmt == "e16":
+                cols = slice(g * NT + lo, g * NT + hi)
+                return e16_codes[j][:, cols].bitcast(FP8X4), e16_plane[j][:, cols]
+            plane, width, base = planes[fmt, j]
+            cols = slice(g * width + base + lo, g * width + base + hi)
+            if fmt == "e8":
+                t, first = e8_tile[j]
+                return t[:, g, first + lo : first + hi].bitcast(FP8X4), plane[E8_PLANE:P, cols]
+            t, first = e4_tile[j]
+            return t[:, g, 2 * (first + lo) : 2 * (first + hi)].bitcast(FP4X4), plane[:, cols]
+
+        def h_operand(g, i0, i1):
+            h = i0 // HALF
+            first = (i0 * PASSES + g) * P if h == 0 else g * NT + (i0 - HALF) * P
+            cols = slice(first, first + (i1 - i0) * P)
+            return h_codes[h][:, cols].bitcast(FP8X4), h_plane[h][:, cols]
+
+        held, part8, total = {}, {}, {}
+
+        def turned(unit):
+            return unit[1] == TURNED_COL and unit[0] >= HALF
+
+        def multiply(fmt, unit):
+            i, j = unit
+            b, acc = take_bank()
+            for g in (1, 0):
+                if turned(unit):
+                    still = e_operand(fmt, g, j, (i - HALF) * P, (i - HALF + 1) * P)
+                    moving = h_operand(g, HALF, ROWS)
+                else:
+                    still = h_operand(g, i, i + 1)
+                    moving = e_operand(fmt, g, j, 0, NT)
                 nc.tensor.matmul_mx(
                     out=acc[:],
-                    lhsT=codes[:, cols].bitcast(FP8X4),
-                    lhsT_scale=plane[:, cols],
-                    rhs=rhs,
-                    rhs_scale=rhs_scale,
-                    start=(g == 0),
-                    stop=(g == PASSES - 1),
+                    lhsT=still[0],
+                    lhsT_scale=still[1],
+                    rhs=moving[0],
+                    rhs_scale=moving[1],
+                    start=(g == 1),
+                    stop=(g == 0),
                 )
-            return acc
+            held[fmt, unit] = (b, acc)
 
-        scaled = {}
+        def new_total(unit):
+            total[unit] = sums.tile([P, NT], F32, name="total", tag="total", bufs=TOTALS)
+            return total[unit]
 
-        def stepped_products(unit, between=None):
-            j, i = divmod(unit, ROWS)
-            t8, b8 = e8_tile[j]
-            t4, b4 = e4_tile[j]
-            r8 = product(
-                i,
-                lambda g: (
-                    t8[:, g, b8 : b8 + NT].bitcast(FP8X4),
-                    e8_plane[E8_PLANE:P, g * N + j * NT : g * N + (j + 1) * NT],
-                ),
-            )
-            r4 = product(
-                i,
-                lambda g: (
-                    t4[:, g, 2 * b4 : 2 * (b4 + NT)].bitcast(FP4X4),
-                    e4_plane[:, g * N + j * NT : g * N + (j + 1) * NT],
-                ),
-            )
-            part8 = sums.tile([P, NT], F32, name="part8", tag="part8", bufs=4)
-            total = sums.tile([P, NT], F32, name="total", tag="total", bufs=14)
-            nc.vector.tensor_tensor(out=part8[:], in0=r8[:], in1=steps[j][:, 0:NT], op=MULT)
-            if between is not None:
-                between()
-            nc.vector.tensor_tensor(out=total[:], in0=r4[:], in1=steps[j][:, NT : 2 * NT], op=MULT)
-            nc.gpsimd.tensor_tensor(out=total[:], in0=total[:], in1=part8[:], op=ADD)
-            scaled[unit] = total
-
-        def plain_product(unit):
-            j, i = divmod(unit, ROWS)
-            r16 = product(i, lambda g: (e16_codes[g, j][0][:].bitcast(FP8X4), e16_codes[g, j][1][:]))
-            total = scaled[unit]
-            if unit % 3 == 1 and unit < UNITS - TAIL:
-                part16 = sums.tile([P, NT], F32, name="part16", tag="part16", bufs=3)
-                nc.scalar.copy(out=part16[:], in_=r16[:])
-                nc.gpsimd.tensor_tensor(out=total[:], in0=total[:], in1=part16[:], op=ADD)
+        def scale8(unit):
+            b, acc = held["e8", unit]
+            if turned(unit):
+                t = total[unit]
+                nc.vector.scalar_tensor_tensor(
+                    out=t[:], in0=acc[:], scalar=step_cols[:, unit[0] - HALF : unit[0] - HALF + 1], in1=t[:], op0=MULT, op1=ADD
+                )
             else:
-                nc.vector.tensor_tensor(out=total[:], in0=r16[:], in1=total[:], op=ADD)
-            nc.sync.dma_start(out=out_rows[i // 2, i % 2, :, j * NT : (j + 1) * NT], in_=total[:])
+                part8[unit] = sums.tile([P, NT], F32, name="part8", tag="part8", bufs=4)
+                nc.vector.tensor_tensor(out=part8[unit][:], in0=acc[:], in1=steps[unit[1]][:, 0:NT], op=MULT)
+            free_banks.append(b)
+
+        def scale4(unit):
+            b, acc = held["e4", unit]
+            t = new_total(unit)
+            if turned(unit):
+                nc.scalar.activation(out=t[:], in_=acc[:], func=COPY, scale=step_cols[:, unit[0] : unit[0] + 1])
+            else:
+                nc.vector.tensor_tensor(out=t[:], in0=acc[:], in1=steps[unit[1]][:, NT : 2 * NT], op=MULT)
+            free_banks.append(b)
+
+        def join(unit, engine):
+            engine.tensor_tensor(out=total[unit][:], in0=total[unit][:], in1=part8[unit][:], op=ADD)
+
+        def store(unit, t):
+            i, j = unit
+            nc.sync.dma_start(out=out_rows[i // 2, i % 2, :, j * NT : (j + 1) * NT], in_=t[:])
+
+        def stepped(unit):
+            if turned(unit):
+                multiply("e4", unit)
+                scale4(unit)
+                multiply("e8", unit)
+                scale8(unit)
+            else:
+                multiply("e8", unit)
+                scale8(unit)
+                multiply("e4", unit)
+                scale4(unit)
+                join(unit, nc.gpsimd)
+
+        def plain(unit):
+            multiply("e16", unit)
+            b, acc = held["e16", unit]
+            if unit in SHED:
+                part16 = sums.tile([P, NT], F32, name="part16", tag="part16", bufs=2)
+                nc.scalar.copy(out=part16[:], in_=acc[:])
+                nc.gpsimd.tensor_tensor(out=total[unit][:], in0=total[unit][:], in1=part16[:], op=ADD)
+            else:
+                nc.vector.tensor_tensor(out=total[unit][:], in0=acc[:], in1=total[unit][:], op=ADD)
+            free_banks.append(b)
+            if not turned(unit):
+                store(unit, total[unit])
+
+        def turn_back(i):
+            b, xt = take_bank()
+            for nb in range(HALF):
+                src = total[HALF + nb, TURNED_COL][:, (i - HALF) * P : (i - HALF + 1) * P]
+                nc.tensor.transpose(xt[:, nb * P : (nb + 1) * P], src, ident[:])
+            t = sums.tile([P, NT], F32, name="turned_back", tag="turned_back", bufs=4)
+            nc.scalar.copy(out=t[:], in_=xt[:])
+            free_banks.append(b)
+            store((i, TURNED_COL), t)
+
+        load_damp()
+        load_gram_row(0)
+        load_steps(0, 1)
+        load_gram_row(1)
+        load_e8(0, 1)
+        load_plane("e8", e8_scales, E8_PLANE, 0, 1)
+        load_e4(0, 1)
+        load_plane("e4", e4_scales, 0, 0, 1)
+        load_gram_pair(1)
+        load_step_rows()
+        load_gram_pair(2)
+        load_gram_pair(3)
+        for g in range(PASSES):
+            load_e16(g, 0, 1)
+        load_steps(1, COLS)
+        load_plane("e8", e8_scales, E8_PLANE, 1, COLS)
+        load_plane("e4", e4_scales, 0, 1, COLS)
+        load_e8(1, COLS)
+        load_e4(1, COLS)
+        for g in range(PASSES):
+            load_e16(g, 1, COLS)
 
         add_damp(0)
         add_damp(1)
-        turn_h(0, [0])
-        turn_h(1, [1])
-        quantise_h([0])
+        turn_h(0)
         spread_steps(0)
-        quantise_h([1])
+        quantise_h_tiles(0, 1)
+        turn_h(1)
+        quantise_h_tiles(1, 2)
+        multiply("e8", (0, 0))
+        scale8((0, 0))
+        multiply("e4", (0, 0))
         add_damp(2)
         add_damp(3)
-        stepped_products(0, lambda: (add_damp(4), add_damp(5)))
-        turn_h(2, [2, 3])
-        turn_h(3, [2, 3])
-        turn_h(4, [4, 5])
-        turn_h(5, [4, 5])
+        scale4((0, 0))
+        multiply("e8", (1, 0))
+        scale8((1, 0))
+        turn_h(2)
+        turn_h(3)
+        widen_step_rows()
+        add_damp(4)
+        add_damp(5)
+        join((0, 0), nc.vector)
+        multiply("e4", (1, 0))
         add_damp(6)
         add_damp(7)
-        quantise_h([2, 3])
-        stepped_products(1)
-        quantise_h([4, 5])
-        turn_h(6, [6, 7])
-        turn_h(7, [6, 7])
-        spread_steps(1)
-        spread_steps(2)
-        stepped_products(2)
-        group_e16(0, 0, 0)
-        group_e16(0, 0, 1)
-        stepped_products(3)
-        quantise_h([6, 7])
-        group_e16(1, 0, 0)
-        group_e16(1, 0, 1)
-        stepped_products(4)
-        stepped_products(5)
-        quantise_e16(0, 0)
-        stepped_products(6)
-        quantise_e16(1, 0)
-        stepped_products(7)
-
-        later = [(g, j) for j in range(1, COLS) for g in range(PASSES)]
+        quantise_h_tiles(2, 4)
+        scale4((1, 0))
+        for i in range(HALF, ROWS):
+            turn_h(i)
+        turn_steps()
+        group_e16(0, 2)
+        group_e16(0, 3)
+        group_e16(0, 0, nc.vector.tensor_copy)
+        quantise_h_by_pass(4)
+        quantise_h_by_pass(5)
+        join((1, 0), nc.vector)
+        quantise_h_by_pass(6)
+        quantise_h_by_pass(7)
+        group_e16(0, 1, nc.vector.tensor_copy)
+        multiply("e8", (2, 0))
+        scale8((2, 0))
+        quantise_e16(0)
+        multiply("e4", (2, 0))
+        scale4((2, 0))
+        join((2, 0), nc.gpsimd)
+        stepped((3, 0))
+        stepped((4, 0))
+        stepped((5, 0))
+        behind = [(i, j) for j in range(COLS) for i in range(ROWS)]
+        ahead = behind[6:]
         done = 0
-        rest = UNITS - ROWS
-        for step in range(rest):
-            if step // 2 < len(later):
-                g, j = later[step // 2]
-                group_e16(g, j, step % 2)
-            want = (step + 1) * (UNITS - TAIL) // rest
-            while done < want - 1:
-                plain_product(done)
-                done = done + 1
-            stepped_products(ROWS + step)
-            if step % 2 == 0 and 0 < step <= 2 * len(later):
-                quantise_e16(*later[step // 2 - 1])
-            while done < want:
-                plain_product(done)
-                done = done + 1
-        while done < UNITS:
-            plain_product(done)
-            done = done + 1
+        for s, unit in enumerate(ahead):
+            if s == 2:
+                spread_steps(1)
+                spread_steps(2)
+            stepped(unit)
+            if s in QUANT:
+                quantise_e16(QUANT[s])
+            if s in GROUP:
+                for j, quarter in GROUP[s]:
+                    group_e16(j, quarter)
+            if s == BACK:
+                for i in range(HALF, ROWS):
+                    turn_back(i)
+            want = (s + 1) * (len(behind) - TAIL) // len(ahead)
+            for late in behind[done:want]:
+                plain(late)
+            done = want
+        for late in behind[done:]:
+            plain(late)

@@ -25,13 +25,13 @@ ROWS = K // P
 HALF = ROWS // 2
 BANKS = 8
 E8_PLANE = 4
+VEC_ROWS = 8
 TURNED_COL = 0
 TOTALS = 16
 TAIL = 3
-BACK = 11
-QUANT = {6: 1, 10: 2}
-SHED = ()
-GROUP = {2 + n: [(1 + n // 4, n % 4)] for n in range(8)}
+BACK = 10
+QUANT = {5: 1, 9: 2}
+GROUP = {1 + n: [(1 + n // 4, n % 4)] for n in range(8)}
 
 
 def tile_damped_gram_error_s10_kernel(
@@ -53,25 +53,25 @@ def tile_damped_gram_error_s10_kernel(
         def kept(name, shape, dtype):
             return keep.tile(shape, dtype, name=name, tag=name, align_bytes=64)
 
+        vec_rows = [kept("vec_rows%d" % n, [P, 2 * P], BF16) for n in range(2)]
+        nc.vector.memset(vec_rows[0][:], 0.0)
         ident = kept("ident", [P, P], F32)
         make_identity(nc, ident[:])
         planes = {}
         for j0, j1 in ((0, 1), (1, COLS)):
             for fmt in ("e8", "e4"):
                 t = kept("%s_plane%d" % (fmt, j0), [P, PASSES * (j1 - j0) * NT], U8)
-                nc.vector.memset(t[:].bitcast(I32), 0)
+                if j0 == 0:
+                    nc.vector.memset(t[:].bitcast(I32), 0)
                 for j in range(j0, j1):
                     planes[fmt, j] = (t, (j1 - j0) * NT, (j - j0) * NT)
         step_rows = kept("step_rows", [P, P], BF16)
         nc.vector.memset(step_rows[:], 0.0)
+        nc.vector.memset(vec_rows[1][:], 0.0)
 
         gram_rows = gram.rearrange("(c p e) k -> c p e k", p=P, e=2)
         out_rows = out.rearrange("(c p e) n -> c e p n", p=P, e=2)
-        damp_sb = kept("damp_sb", [P, HALF, 2], BF16)
-        g_tile, e8_tile, e4_tile, e16_tile, step_words = {}, {}, {}, {}, {}
-
-        def load_damp():
-            nc.sync.dma_start(out=damp_sb[:], in_=damp.rearrange("(c p e) -> p c e", p=P, e=2))
+        g_tile, e8_tile, e4_tile, e16_tile = {}, {}, {}, {}
 
         def load_gram_row(i):
             t = kept("gram%d" % i, [P, K], BF16)
@@ -112,12 +112,9 @@ def tile_damped_gram_error_s10_kernel(
             for j in range(j0, j1):
                 e16_tile[g, j] = (t, (j - j0) * NT)
 
-        def load_steps(j0, j1):
-            for v, step in enumerate((step8, step4)):
-                t = kept("step_words%d_%d" % (v, j0), [P, j1 - j0, 4], BF16)
-                nc.sync.dma_start(out=t[:], in_=step.rearrange("(j p c) -> p j c", p=P, c=4)[:, j0:j1, :])
-                for j in range(j0, j1):
-                    step_words[v, j] = (t, j - j0)
+        def load_rows(n, first, vec, r0, r1):
+            rows = vec.rearrange("(r w) -> r w", w=2 * P)[r0:r1]
+            nc.sync.dma_start(out=vec_rows[n][first : first + r1 - r0, :], in_=rows)
 
         def load_step_rows():
             for v, step in enumerate((step8, step4)):
@@ -128,26 +125,47 @@ def tile_damped_gram_error_s10_kernel(
         h_codes = [kept("h_codes%d" % h, [P, PASSES * NT], U32) for h in range(2)]
         h_plane = [kept("h_plane%d" % h, [P, PASSES * NT], U8) for h in range(2)]
 
+        vec_cols = [kept("vec_cols%d" % n, [P, VEC_ROWS], F32) for n in range(2)]
+
+        def turn_vectors(n):
+            b, xt = take_bank()
+            nc.tensor.transpose(xt[:, 0:P], vec_rows[n][:].bitcast(F32), ident[:])
+            nc.scalar.copy(out=vec_cols[n][:], in_=xt[:, 0:VEC_ROWS])
+            free_banks.append(b)
+
         def add_damp(i):
             t, base = g_tile[i]
             c, e = divmod(i, 2)
             diag = t[:, base + 2 * P * c + e : base + 2 * P * (c + 1) : 2]
+            col = 2 * c + e
             nc.vector.scalar_tensor_tensor(
-                out=diag, in0=ident[:], scalar=damp_sb[:, c, e : e + 1], in1=diag, op0=MULT, op1=ADD
+                out=diag, in0=ident[:], scalar=vec_cols[0][:].bitcast(BF16)[:, col : col + 1], in1=diag, op0=MULT, op1=ADD
             )
 
-        def turn_h(i):
+        h_bank = {}
+
+        def turn_h_pass(i, g):
             t, base = g_tile[i]
             words = t[:].bitcast(F32)
-            b, xt = take_bank()
-            for g in (1, 0):
-                for u in range(2):
-                    lo = base // 2 + 2 * P * g
-                    slot = 2 * g + u
-                    nc.tensor.transpose(xt[:, slot * P : (slot + 1) * P], words[:, lo + u : lo + 2 * P : 2], ident[:])
+            if i not in h_bank:
+                h_bank[i] = take_bank()
+            xt = h_bank[i][1]
+            for u in range(2):
+                lo = base // 2 + 2 * P * g
+                slot = 2 * g + u
+                nc.tensor.transpose(xt[:, slot * P : (slot + 1) * P], words[:, lo + u : lo + 2 * P : 2], ident[:])
+
+        def group_h(i, g0=0, g1=PASSES):
+            b, xt = h_bank.pop(i)
             dst = h_grouped[i // HALF][:].bitcast(F32).rearrange("p (i g m u) -> p i g m u", g=PASSES, i=HALF, u=2)
-            nc.scalar.copy(out=dst[:, i % HALF], in_=xt[:].rearrange("p (g u m) -> p g m u", g=PASSES, u=2))
+            src = xt[:].rearrange("p (g u m) -> p g m u", g=PASSES, u=2)
+            nc.scalar.copy(out=dst[:, i % HALF, g0:g1], in_=src[:, g0:g1])
             free_banks.append(b)
+
+        def turn_h(i):
+            for g in (1, 0) if i < HALF else (0, 1):
+                turn_h_pass(i, g)
+            group_h(i)
 
         def quantise_h(h, lo, hi, source):
             nc.vector.quantize_mx(
@@ -170,19 +188,14 @@ def tile_damped_gram_error_s10_kernel(
         def spread_steps(j):
             b, xt = take_bank()
             for v in range(2):
-                t, row = step_words[v, j]
-                cols = t[:].rearrange("p j c -> p (j c)").bitcast(F32)
                 for c in range(2):
-                    w = 2 * row + c
+                    col = HALF + 2 * v + c if j == 0 else 4 * v + 2 * (j - 1) + c
                     slot = 2 * v + c
                     nc.tensor.transpose(
-                        xt[:, slot * P : (slot + 1) * P], cols[:, w : w + 1].to_broadcast([P, P]), ident[:]
+                        xt[:, slot * P : (slot + 1) * P], vec_cols[min(j, 1)][:, col : col + 1].to_broadcast([P, P]), ident[:]
                     )
             steps[j] = kept("steps%d" % j, [P, 2 * NT], BF16)
-            nc.scalar.copy(
-                out=steps[j][:].bitcast(F32).rearrange("p (v n c) -> p v n c", v=2, c=2),
-                in_=xt[:].rearrange("p (v c n) -> p v n c", v=2, c=2),
-            )
+            nc.scalar.copy(out=steps[j][:].bitcast(F32), in_=xt[:])
             free_banks.append(b)
 
         step_rows32 = kept("step_rows32", [P, P], F32)
@@ -274,8 +287,8 @@ def tile_damped_gram_error_s10_kernel(
                     out=t[:], in0=acc[:], scalar=step_cols[:, unit[0] - HALF : unit[0] - HALF + 1], in1=t[:], op0=MULT, op1=ADD
                 )
             else:
-                part8[unit] = sums.tile([P, NT], F32, name="part8", tag="part8", bufs=4)
-                nc.vector.tensor_tensor(out=part8[unit][:], in0=acc[:], in1=steps[unit[1]][:, 0:NT], op=MULT)
+                part8[unit] = sums.tile([P, NT], F32, name="part8", tag="part8", bufs=6)
+                nc.vector.tensor_tensor(out=part8[unit][:], in0=steps[unit[1]][:, 0:NT], in1=acc[:], op=MULT)
             free_banks.append(b)
 
         def scale4(unit):
@@ -284,7 +297,7 @@ def tile_damped_gram_error_s10_kernel(
             if turned(unit):
                 nc.scalar.activation(out=t[:], in_=acc[:], func=COPY, scale=step_cols[:, unit[0] : unit[0] + 1])
             else:
-                nc.vector.tensor_tensor(out=t[:], in0=acc[:], in1=steps[unit[1]][:, NT : 2 * NT], op=MULT)
+                nc.vector.tensor_tensor(out=t[:], in0=steps[unit[1]][:, NT : 2 * NT], in1=acc[:], op=MULT)
             free_banks.append(b)
 
         def join(unit, engine):
@@ -310,12 +323,7 @@ def tile_damped_gram_error_s10_kernel(
         def plain(unit):
             multiply("e16", unit)
             b, acc = held["e16", unit]
-            if unit in SHED:
-                part16 = sums.tile([P, NT], F32, name="part16", tag="part16", bufs=2)
-                nc.scalar.copy(out=part16[:], in_=acc[:])
-                nc.gpsimd.tensor_tensor(out=total[unit][:], in0=total[unit][:], in1=part16[:], op=ADD)
-            else:
-                nc.vector.tensor_tensor(out=total[unit][:], in0=acc[:], in1=total[unit][:], op=ADD)
+            nc.vector.tensor_tensor(out=total[unit][:], in0=total[unit][:], in1=acc[:], op=ADD)
             free_banks.append(b)
             if not turned(unit):
                 store(unit, total[unit])
@@ -330,73 +338,88 @@ def tile_damped_gram_error_s10_kernel(
             free_banks.append(b)
             store((i, TURNED_COL), t)
 
-        load_damp()
         load_gram_row(0)
-        load_steps(0, 1)
+        load_rows(0, 0, damp, 0, HALF)
+        load_rows(0, HALF, step8, 0, 2)
+        load_rows(0, HALF + 2, step4, 0, 2)
         load_gram_row(1)
         load_e8(0, 1)
         load_plane("e8", e8_scales, E8_PLANE, 0, 1)
         load_e4(0, 1)
         load_plane("e4", e4_scales, 0, 0, 1)
         load_gram_pair(1)
-        load_step_rows()
         load_gram_pair(2)
         load_gram_pair(3)
+        load_step_rows()
+        load_rows(1, 0, step8, 2, 6)
+        load_rows(1, 4, step4, 2, 6)
         for g in range(PASSES):
             load_e16(g, 0, 1)
-        load_steps(1, COLS)
+
+        turn_vectors(0)
+        turn_h_pass(0, 1)
+        group_h(0, 1, 2)
+        add_damp(0)
+        spread_steps(0)
+        turn_h_pass(0, 0)
+        group_h(0, 0, 1)
+        quantise_h(0, P, 2 * P, P)
+        add_damp(1)
+        quantise_h(0, 0, P, 0)
+        for fmt in ("e8", "e4"):
+            nc.vector.memset(planes[fmt, 1][0][:].bitcast(I32), 0)
         load_plane("e8", e8_scales, E8_PLANE, 1, COLS)
         load_plane("e4", e4_scales, 0, 1, COLS)
         load_e8(1, COLS)
         load_e4(1, COLS)
-        for g in range(PASSES):
-            load_e16(g, 1, COLS)
-
-        add_damp(0)
-        add_damp(1)
-        turn_h(0)
-        spread_steps(0)
-        quantise_h_tiles(0, 1)
+        for j in range(1, COLS):
+            for g in range(PASSES):
+                load_e16(g, j, j + 1)
         turn_h(1)
-        quantise_h_tiles(1, 2)
         multiply("e8", (0, 0))
-        scale8((0, 0))
-        multiply("e4", (0, 0))
+        quantise_h_tiles(1, 2)
         add_damp(2)
         add_damp(3)
+        scale8((0, 0))
+        multiply("e4", (0, 0))
         scale4((0, 0))
-        multiply("e8", (1, 0))
-        scale8((1, 0))
         turn_h(2)
         turn_h(3)
         widen_step_rows()
         add_damp(4)
         add_damp(5)
-        join((0, 0), nc.vector)
-        multiply("e4", (1, 0))
+        multiply("e8", (1, 0))
         add_damp(6)
         add_damp(7)
         quantise_h_tiles(2, 4)
+        scale8((1, 0))
+        multiply("e4", (1, 0))
         scale4((1, 0))
-        for i in range(HALF, ROWS):
-            turn_h(i)
-        turn_steps()
-        group_e16(0, 2)
-        group_e16(0, 3)
+        turn_h(4)
+        turn_h(5)
         group_e16(0, 0, nc.vector.tensor_copy)
         quantise_h_by_pass(4)
         quantise_h_by_pass(5)
-        join((1, 0), nc.vector)
-        quantise_h_by_pass(6)
-        quantise_h_by_pass(7)
-        group_e16(0, 1, nc.vector.tensor_copy)
         multiply("e8", (2, 0))
+        group_e16(0, 1, nc.vector.tensor_copy)
         scale8((2, 0))
-        quantise_e16(0)
         multiply("e4", (2, 0))
         scale4((2, 0))
-        join((2, 0), nc.gpsimd)
-        stepped((3, 0))
+        group_e16(0, 2)
+        turn_h(6)
+        turn_h(7)
+        turn_steps()
+        turn_vectors(1)
+        group_e16(0, 3)
+        quantise_h_by_pass(6)
+        quantise_h_by_pass(7)
+        multiply("e8", (3, 0))
+        scale8((3, 0))
+        multiply("e4", (3, 0))
+        quantise_e16(0)
+        scale4((3, 0))
+        for i in (3, 0, 1, 2):
+            join((i, 0), nc.gpsimd)
         stepped((4, 0))
         stepped((5, 0))
         behind = [(i, j) for j in range(COLS) for i in range(ROWS)]

@@ -18,26 +18,32 @@ ADD = mybir.AluOpType.add
 COPY = mybir.ActivationFunctionType.Copy
 
 P = 128
-PASSES = 2
+PACK = 4
+QUADRANT = 32
+PASSES = K // (P * PACK)
 NT = 512
 COLS = N // NT
 ROWS = K // P
 HALF = ROWS // 2
 BANKS = 8
+QUARTER = NT // 2
 E8_PLANE = 4
-VEC_ROWS = 8
-TURNED_COL = 0
-TOTALS = 16
+
+FIRST_ROUND_UNIT = 6
 TAIL = 3
-BACK = 10
-QUANT = {5: 1, 9: 2}
-GROUP = {1 + n: [(1 + n // 4, n % 4)] for n in range(8)}
+FIRST_GROUPING_ROUND = 1
+QUANTISE_ROUND = {5: 1, 11: 2}
+TURN_BACK_ROUND = 11
+SUM_BUFS = 18
+PART_BUFS = 6
+TURNED_BACK_BUFS = HALF
 
 
 def tile_damped_gram_error_s10_kernel(
     tc, gram, damp, e4_words, e4_scales, e8_words, e8_scales, e16, step4, step8, out
 ):
     nc = tc.nc
+    step_vectors = (step8, step4)
     with ExitStack() as ctx:
         keep = ctx.enter_context(tc.tile_pool(name="keep", bufs=1))
         sums = ctx.enter_context(tc.tile_pool(name="sums", bufs=1))
@@ -53,40 +59,43 @@ def tile_damped_gram_error_s10_kernel(
         def kept(name, shape, dtype):
             return keep.tile(shape, dtype, name=name, tag=name, align_bytes=64)
 
-        vec_rows = [kept("vec_rows%d" % n, [P, 2 * P], BF16) for n in range(2)]
-        nc.vector.memset(vec_rows[0][:], 0.0)
         ident = kept("ident", [P, P], F32)
         make_identity(nc, ident[:])
+
         planes = {}
         for j0, j1 in ((0, 1), (1, COLS)):
-            for fmt in ("e8", "e4"):
-                t = kept("%s_plane%d" % (fmt, j0), [P, PASSES * (j1 - j0) * NT], U8)
-                if j0 == 0:
-                    nc.vector.memset(t[:].bitcast(I32), 0)
+            for part in ("e8", "e4"):
+                t = kept("%s_plane%d" % (part, j0), [P, PASSES * (j1 - j0) * NT], U8)
                 for j in range(j0, j1):
-                    planes[fmt, j] = (t, (j1 - j0) * NT, (j - j0) * NT)
+                    planes[part, j] = (t, (j1 - j0) * NT, (j - j0) * NT)
+
+        def zero_planes(j0):
+            for part in ("e8", "e4"):
+                nc.vector.memset(planes[part, j0][0][:].bitcast(I32), 0)
+
+        zero_planes(0)
         step_rows = kept("step_rows", [P, P], BF16)
         nc.vector.memset(step_rows[:], 0.0)
-        nc.vector.memset(vec_rows[1][:], 0.0)
 
         gram_rows = gram.rearrange("(c p e) k -> c p e k", p=P, e=2)
         out_rows = out.rearrange("(c p e) n -> c e p n", p=P, e=2)
-        g_tile, e8_tile, e4_tile, e16_tile = {}, {}, {}, {}
+        damp_cols = kept("damp_cols", [P, HALF, 2], BF16)
+        gram_tile, e8_tile, e4_tile, e16_tile, step_words = {}, {}, {}, {}, []
 
         def load_gram_row(i):
             t = kept("gram%d" % i, [P, K], BF16)
             nc.sync.dma_start(out=t[:], in_=gram_rows[i // 2, :, i % 2, :])
-            g_tile[i] = (t, 0)
+            gram_tile[i] = (t, 0)
 
         def load_gram_pair(c):
             t = kept("gram%d" % (2 * c), [P, 2 * K], BF16)
             nc.sync.dma_start(out=t[:], in_=gram_rows[c].rearrange("p e k -> p (e k)"))
-            g_tile[2 * c] = (t, 0)
-            g_tile[2 * c + 1] = (t, K)
+            gram_tile[2 * c] = (t, 0)
+            gram_tile[2 * c + 1] = (t, K)
 
         def load_e8(j0, j1):
             t = kept("e8_codes%d" % j0, [P, PASSES, (j1 - j0) * NT], U32)
-            src = e8_words.rearrange("g p n t -> p g (n t)")[:, :, 4 * NT * j0 : 4 * NT * j1]
+            src = e8_words.rearrange("g p n t -> p g (n t)")[:, :, PACK * NT * j0 : PACK * NT * j1]
             nc.sync.dma_start(out=t[:].bitcast(I32), in_=src.bitcast(I32))
             for j in range(j0, j1):
                 e8_tile[j] = (t, (j - j0) * NT)
@@ -98,146 +107,131 @@ def tile_damped_gram_error_s10_kernel(
             for j in range(j0, j1):
                 e4_tile[j] = (t, (j - j0) * NT)
 
-        def load_plane(fmt, scales, first, j0, j1):
-            plane = planes[fmt, j0][0]
+        def load_plane(part, scales, first, j0, j1):
+            plane = planes[part, j0][0]
             rows = scales.bitcast(I32).rearrange("g (q r) n -> r q g n", r=4)[:, :, :, NT // 4 * j0 : NT // 4 * j1]
             for r in range(4):
-                dst = plane[:].bitcast(I32)[first + r : P : 32, :]
+                dst = plane[:].bitcast(I32)[first + r : P : QUADRANT, :]
                 nc.sync.dma_start(out=dst.rearrange("q (g n) -> q g n", g=PASSES), in_=rows[r])
 
-        def load_e16(g, j0, j1):
-            t = kept("e16_raw%d_%d" % (g, j0), [P, 4, (j1 - j0) * NT], BF16)
-            src = e16.rearrange("(g p t) n -> g p t n", p=P, t=4)[g, :, :, NT * j0 : NT * j1]
-            nc.sync.dma_start(out=t[:], in_=src)
-            for j in range(j0, j1):
-                e16_tile[g, j] = (t, (j - j0) * NT)
+        def load_e16(j):
+            for g in range(PASSES):
+                t = kept("e16_raw%d_%d" % (g, j), [P, PACK, NT], BF16)
+                src = e16.rearrange("(g p t) n -> g p t n", p=P, t=PACK)[g, :, :, NT * j : NT * (j + 1)]
+                nc.sync.dma_start(out=t[:], in_=src)
+                e16_tile[g, j] = t
 
-        def load_rows(n, first, vec, r0, r1):
-            rows = vec.rearrange("(r w) -> r w", w=2 * P)[r0:r1]
-            nc.sync.dma_start(out=vec_rows[n][first : first + r1 - r0, :], in_=rows)
+        def load_step_words():
+            for v, step in enumerate(step_vectors):
+                t = kept("step_words%d" % v, [P, 1, 4], BF16)
+                nc.sync.dma_start(out=t[:], in_=step.rearrange("(j p c) -> p j c", p=P, c=4)[:, 0:1, :])
+                step_words.append(t)
 
         def load_step_rows():
-            for v, step in enumerate((step8, step4)):
-                rows = step.rearrange("(j b p) -> j b p", b=4, p=P)[TURNED_COL]
-                nc.sync.dma_start(out=step_rows[4 * v : 4 * v + 4, :], in_=rows)
+            for v, step in enumerate(step_vectors):
+                rows = step.rearrange("(j b p) -> j b p", b=HALF, p=P)[0]
+                nc.sync.dma_start(out=step_rows[HALF * v : HALF * (v + 1), :], in_=rows)
 
         h_grouped = [kept("h_grouped%d" % h, [P, HALF * K], BF16) for h in range(2)]
         h_codes = [kept("h_codes%d" % h, [P, PASSES * NT], U32) for h in range(2)]
         h_plane = [kept("h_plane%d" % h, [P, PASSES * NT], U8) for h in range(2)]
 
-        vec_cols = [kept("vec_cols%d" % n, [P, VEC_ROWS], F32) for n in range(2)]
-
-        def turn_vectors(n):
-            b, xt = take_bank()
-            nc.tensor.transpose(xt[:, 0:P], vec_rows[n][:].bitcast(F32), ident[:])
-            nc.scalar.copy(out=vec_cols[n][:], in_=xt[:, 0:VEC_ROWS])
-            free_banks.append(b)
-
         def add_damp(i):
-            t, base = g_tile[i]
+            t, base = gram_tile[i]
             c, e = divmod(i, 2)
             diag = t[:, base + 2 * P * c + e : base + 2 * P * (c + 1) : 2]
-            col = 2 * c + e
             nc.vector.scalar_tensor_tensor(
-                out=diag, in0=ident[:], scalar=vec_cols[0][:].bitcast(BF16)[:, col : col + 1], in1=diag, op0=MULT, op1=ADD
+                out=diag, in0=ident[:], scalar=damp_cols[:, c, e : e + 1], in1=diag, op0=MULT, op1=ADD
             )
 
-        h_bank = {}
-
-        def turn_h_pass(i, g):
-            t, base = g_tile[i]
-            words = t[:].bitcast(F32)
-            if i not in h_bank:
-                h_bank[i] = take_bank()
-            xt = h_bank[i][1]
-            for u in range(2):
-                lo = base // 2 + 2 * P * g
-                slot = 2 * g + u
-                nc.tensor.transpose(xt[:, slot * P : (slot + 1) * P], words[:, lo + u : lo + 2 * P : 2], ident[:])
-
-        def group_h(i, g0=0, g1=PASSES):
-            b, xt = h_bank.pop(i)
-            dst = h_grouped[i // HALF][:].bitcast(F32).rearrange("p (i g m u) -> p i g m u", g=PASSES, i=HALF, u=2)
-            src = xt[:].rearrange("p (g u m) -> p g m u", g=PASSES, u=2)
-            nc.scalar.copy(out=dst[:, i % HALF, g0:g1], in_=src[:, g0:g1])
-            free_banks.append(b)
-
         def turn_h(i):
+            t, base = gram_tile[i]
+            words = t[:].bitcast(F32)
+            b, turned_words = take_bank()
             for g in (1, 0) if i < HALF else (0, 1):
-                turn_h_pass(i, g)
-            group_h(i)
+                first = base // 2 + 2 * P * g
+                for u in range(2):
+                    place = slice((2 * g + u) * P, (2 * g + u + 1) * P)
+                    nc.tensor.transpose(turned_words[:, place], words[:, first + u : first + 2 * P : 2], ident[:])
+            dst = h_grouped[i // HALF][:].bitcast(F32).rearrange("p (i g m u) -> p i g m u", g=PASSES, i=HALF, u=2)
+            src = turned_words[:].rearrange("p (g u m) -> p g m u", g=PASSES, u=2)
+            nc.scalar.copy(out=dst[:, i % HALF], in_=src)
+            free_banks.append(b)
 
         def quantise_h(h, lo, hi, source):
             nc.vector.quantize_mx(
                 out=h_codes[h][:, lo:hi].bitcast(FP8X4),
                 scales=h_plane[h][:, lo:hi],
-                in_=h_grouped[h][:, 4 * source : 4 * (source + hi - lo)],
+                in_=h_grouped[h][:, PACK * source : PACK * (source + hi - lo)],
             )
 
-        def quantise_h_tiles(i0, i1):
+        def quantise_first_half(i0, i1):
             quantise_h(0, i0 * PASSES * P, i1 * PASSES * P, i0 * PASSES * P)
 
-        def quantise_h_by_pass(i):
+        def quantise_second_half(i):
             for g in (1, 0):
                 lo = g * NT + (i - HALF) * P
                 quantise_h(1, lo, lo + P, ((i - HALF) * PASSES + g) * P)
 
-        steps = {}
-        step_cols = kept("step_cols", [P, 8], F32)
+        spread_steps = {}
+        step_cols = kept("step_cols", [P, 2 * HALF], F32)
 
-        def spread_steps(j):
-            b, xt = take_bank()
+        def spread_first_steps():
+            b, spread = take_bank()
             for v in range(2):
-                for c in range(2):
-                    col = HALF + 2 * v + c if j == 0 else 4 * v + 2 * (j - 1) + c
-                    slot = 2 * v + c
-                    nc.tensor.transpose(
-                        xt[:, slot * P : (slot + 1) * P], vec_cols[min(j, 1)][:, col : col + 1].to_broadcast([P, P]), ident[:]
-                    )
-            steps[j] = kept("steps%d" % j, [P, 2 * NT], BF16)
-            nc.scalar.copy(out=steps[j][:].bitcast(F32), in_=xt[:])
+                words = step_words[v][:].rearrange("p j c -> p (j c)").bitcast(F32)
+                for w in range(2):
+                    place = slice((2 * v + w) * P, (2 * v + w + 1) * P)
+                    nc.tensor.transpose(spread[:, place], words[:, w : w + 1].to_broadcast([P, P]), ident[:])
+            both = kept("steps0", [P, 2 * NT], BF16)
+            spread_steps[0] = [both[:, 0:NT], both[:, NT : 2 * NT]]
+            nc.scalar.copy(
+                out=both[:].bitcast(F32).rearrange("p (v n w) -> p v n w", v=2, w=2),
+                in_=spread[:].rearrange("p (v w n) -> p v n w", v=2, w=2),
+            )
             free_banks.append(b)
+
+        def load_spread_steps(j):
+            tiles = [kept("steps%d_%d" % (j, v), [P, NT], BF16) for v in range(2)]
+            spread_steps[j] = [t[:] for t in tiles]
+            for t, step in zip(tiles, step_vectors):
+                nc.sync.dma_start(out=t[:], in_=step[j * NT : (j + 1) * NT].partition_broadcast(P))
 
         step_rows32 = kept("step_rows32", [P, P], F32)
 
-        def widen_step_rows():
-            nc.scalar.copy(out=step_rows32[:], in_=step_rows[:])
-
-        def turn_steps():
-            b, xt = take_bank()
-            nc.tensor.transpose(xt[:, 0:P], step_rows32[:], ident[:])
-            nc.scalar.copy(out=step_cols[:], in_=xt[:, 0:8])
+        def turn_step_rows():
+            b, turned_rows = take_bank()
+            nc.tensor.transpose(turned_rows[:, 0:P], step_rows32[:], ident[:])
+            nc.scalar.copy(out=step_cols[:], in_=turned_rows[:, 0 : 2 * HALF])
             free_banks.append(b)
 
-        e16_grouped = [kept("e16_grouped%d" % j, [P, PASSES * 4 * NT], BF16) for j in range(COLS)]
+        e16_grouped = [kept("e16_grouped%d" % j, [P, PASSES * PACK * NT], BF16) for j in range(COLS)]
         e16_codes = [kept("e16_codes%d" % j, [P, PASSES * NT], U32) for j in range(COLS)]
         e16_plane = [kept("e16_plane%d" % j, [P, PASSES * NT], U8) for j in range(COLS)]
 
-        def group_e16(j, quarter, copy=nc.scalar.copy):
-            g, half = divmod(quarter, 2)
-            raw, base = e16_tile[g, j]
-            w = NT // 2
-            dst = e16_grouped[j][:, 4 * w * quarter : 4 * w * (quarter + 1)]
-            src = raw[:, :, base + w * half : base + w * (half + 1)]
+        def group_e16(j, quarter, copy):
+            g, side = divmod(quarter, 2)
+            dst = e16_grouped[j][:, PACK * QUARTER * quarter : PACK * QUARTER * (quarter + 1)]
+            src = e16_tile[g, j][:, :, QUARTER * side : QUARTER * (side + 1)]
             copy(
-                out=dst.rearrange("p (c i t) -> p c t i", i=4, t=4),
+                out=dst.rearrange("p (c i t) -> p c t i", i=4, t=PACK),
                 in_=src.rearrange("p t (c i) -> p c t i", i=4),
             )
 
-        def quantise_e16(j, g0=0, g1=PASSES):
+        def quantise_e16(j, g0, g1):
             nc.vector.quantize_mx(
                 out=e16_codes[j][:, g0 * NT : g1 * NT].bitcast(FP8X4),
                 scales=e16_plane[j][:, g0 * NT : g1 * NT],
-                in_=e16_grouped[j][:, 4 * g0 * NT : 4 * g1 * NT],
+                in_=e16_grouped[j][:, PACK * g0 * NT : PACK * g1 * NT],
             )
 
-        def e_operand(fmt, g, j, lo, hi):
-            if fmt == "e16":
+        def error_operand(part, g, j, lo, hi):
+            if part == "e16":
                 cols = slice(g * NT + lo, g * NT + hi)
                 return e16_codes[j][:, cols].bitcast(FP8X4), e16_plane[j][:, cols]
-            plane, width, base = planes[fmt, j]
+            plane, width, base = planes[part, j]
             cols = slice(g * width + base + lo, g * width + base + hi)
-            if fmt == "e8":
+            if part == "e8":
                 t, first = e8_tile[j]
                 return t[:, g, first + lo : first + hi].bitcast(FP8X4), plane[E8_PLANE:P, cols]
             t, first = e4_tile[j]
@@ -249,55 +243,53 @@ def tile_damped_gram_error_s10_kernel(
             cols = slice(first, first + (i1 - i0) * P)
             return h_codes[h][:, cols].bitcast(FP8X4), h_plane[h][:, cols]
 
-        held, part8, total = {}, {}, {}
+        product, part8, total = {}, {}, {}
 
         def turned(unit):
-            return unit[1] == TURNED_COL and unit[0] >= HALF
+            return unit[1] == 0 and unit[0] >= HALF
 
-        def multiply(fmt, unit):
+        def multiply(part, unit):
             i, j = unit
             b, acc = take_bank()
             for g in (1, 0):
                 if turned(unit):
-                    still = e_operand(fmt, g, j, (i - HALF) * P, (i - HALF + 1) * P)
+                    stationary = error_operand(part, g, j, (i - HALF) * P, (i - HALF + 1) * P)
                     moving = h_operand(g, HALF, ROWS)
                 else:
-                    still = h_operand(g, i, i + 1)
-                    moving = e_operand(fmt, g, j, 0, NT)
+                    stationary = h_operand(g, i, i + 1)
+                    moving = error_operand(part, g, j, 0, NT)
                 nc.tensor.matmul_mx(
                     out=acc[:],
-                    lhsT=still[0],
-                    lhsT_scale=still[1],
+                    lhsT=stationary[0],
+                    lhsT_scale=stationary[1],
                     rhs=moving[0],
                     rhs_scale=moving[1],
                     start=(g == 1),
                     stop=(g == 0),
                 )
-            held[fmt, unit] = (b, acc)
-
-        def new_total(unit):
-            total[unit] = sums.tile([P, NT], F32, name="total", tag="total", bufs=TOTALS)
-            return total[unit]
+            product[part, unit] = (b, acc)
 
         def scale8(unit):
-            b, acc = held["e8", unit]
+            i, j = unit
+            b, acc = product["e8", unit]
             if turned(unit):
-                t = total[unit]
+                step_col = step_cols[:, i - HALF : i - HALF + 1]
                 nc.vector.scalar_tensor_tensor(
-                    out=t[:], in0=acc[:], scalar=step_cols[:, unit[0] - HALF : unit[0] - HALF + 1], in1=t[:], op0=MULT, op1=ADD
+                    out=total[unit][:], in0=acc[:], scalar=step_col, in1=total[unit][:], op0=MULT, op1=ADD
                 )
             else:
-                part8[unit] = sums.tile([P, NT], F32, name="part8", tag="part8", bufs=6)
-                nc.vector.tensor_tensor(out=part8[unit][:], in0=steps[unit[1]][:, 0:NT], in1=acc[:], op=MULT)
+                part8[unit] = sums.tile([P, NT], F32, name="part8", tag="part8", bufs=PART_BUFS)
+                nc.vector.tensor_tensor(out=part8[unit][:], in0=acc[:], in1=spread_steps[j][0], op=MULT)
             free_banks.append(b)
 
         def scale4(unit):
-            b, acc = held["e4", unit]
-            t = new_total(unit)
+            i, j = unit
+            b, acc = product["e4", unit]
+            total[unit] = sums.tile([P, NT], F32, name="total", tag="total", bufs=SUM_BUFS)
             if turned(unit):
-                nc.scalar.activation(out=t[:], in_=acc[:], func=COPY, scale=step_cols[:, unit[0] : unit[0] + 1])
+                nc.scalar.activation(out=total[unit][:], in_=acc[:], func=COPY, scale=step_cols[:, i : i + 1])
             else:
-                nc.vector.tensor_tensor(out=t[:], in0=steps[unit[1]][:, NT : 2 * NT], in1=acc[:], op=MULT)
+                nc.vector.tensor_tensor(out=total[unit][:], in0=acc[:], in1=spread_steps[j][1], op=MULT)
             free_banks.append(b)
 
         def join(unit, engine):
@@ -307,7 +299,7 @@ def tile_damped_gram_error_s10_kernel(
             i, j = unit
             nc.sync.dma_start(out=out_rows[i // 2, i % 2, :, j * NT : (j + 1) * NT], in_=t[:])
 
-        def stepped(unit):
+        def stepped_products(unit):
             if turned(unit):
                 multiply("e4", unit)
                 scale4(unit)
@@ -320,127 +312,112 @@ def tile_damped_gram_error_s10_kernel(
                 scale4(unit)
                 join(unit, nc.gpsimd)
 
-        def plain(unit):
+        def e16_product(unit):
             multiply("e16", unit)
-            b, acc = held["e16", unit]
-            nc.vector.tensor_tensor(out=total[unit][:], in0=total[unit][:], in1=acc[:], op=ADD)
+            b, acc = product["e16", unit]
+            nc.vector.tensor_tensor(out=total[unit][:], in0=acc[:], in1=total[unit][:], op=ADD)
             free_banks.append(b)
             if not turned(unit):
                 store(unit, total[unit])
 
         def turn_back(i):
-            b, xt = take_bank()
-            for nb in range(HALF):
-                src = total[HALF + nb, TURNED_COL][:, (i - HALF) * P : (i - HALF + 1) * P]
-                nc.tensor.transpose(xt[:, nb * P : (nb + 1) * P], src, ident[:])
-            t = sums.tile([P, NT], F32, name="turned_back", tag="turned_back", bufs=4)
-            nc.scalar.copy(out=t[:], in_=xt[:])
+            b, straight = take_bank()
+            for block in range(HALF):
+                src = total[HALF + block, 0][:, (i - HALF) * P : (i - HALF + 1) * P]
+                nc.tensor.transpose(straight[:, block * P : (block + 1) * P], src, ident[:])
+            t = sums.tile([P, NT], F32, name="turned_back", tag="turned_back", bufs=TURNED_BACK_BUFS)
+            nc.scalar.copy(out=t[:], in_=straight[:])
             free_banks.append(b)
-            store((i, TURNED_COL), t)
+            store((i, 0), t)
 
+        nc.sync.dma_start(out=damp_cols[:], in_=damp.rearrange("(c p e) -> p c e", p=P, e=2))
         load_gram_row(0)
-        load_rows(0, 0, damp, 0, HALF)
-        load_rows(0, HALF, step8, 0, 2)
-        load_rows(0, HALF + 2, step4, 0, 2)
+        load_step_words()
         load_gram_row(1)
         load_e8(0, 1)
         load_plane("e8", e8_scales, E8_PLANE, 0, 1)
         load_e4(0, 1)
         load_plane("e4", e4_scales, 0, 0, 1)
         load_gram_pair(1)
+        load_step_rows()
         load_gram_pair(2)
         load_gram_pair(3)
-        load_step_rows()
-        load_rows(1, 0, step8, 2, 6)
-        load_rows(1, 4, step4, 2, 6)
-        for g in range(PASSES):
-            load_e16(g, 0, 1)
+        load_e16(0)
 
-        turn_vectors(0)
-        turn_h_pass(0, 1)
-        group_h(0, 1, 2)
         add_damp(0)
-        spread_steps(0)
-        turn_h_pass(0, 0)
-        group_h(0, 0, 1)
-        quantise_h(0, P, 2 * P, P)
         add_damp(1)
-        quantise_h(0, 0, P, 0)
-        for fmt in ("e8", "e4"):
-            nc.vector.memset(planes[fmt, 1][0][:].bitcast(I32), 0)
+        turn_h(0)
+        spread_first_steps()
+        quantise_first_half(0, 1)
+
+        zero_planes(1)
         load_plane("e8", e8_scales, E8_PLANE, 1, COLS)
         load_plane("e4", e4_scales, 0, 1, COLS)
         load_e8(1, COLS)
         load_e4(1, COLS)
         for j in range(1, COLS):
-            for g in range(PASSES):
-                load_e16(g, j, j + 1)
+            load_spread_steps(j)
+            load_e16(j)
+
         turn_h(1)
+        quantise_first_half(1, 2)
+
         multiply("e8", (0, 0))
-        quantise_h_tiles(1, 2)
-        add_damp(2)
-        add_damp(3)
         scale8((0, 0))
         multiply("e4", (0, 0))
+        add_damp(2)
+        add_damp(3)
         scale4((0, 0))
+        multiply("e8", (1, 0))
+        scale8((1, 0))
         turn_h(2)
         turn_h(3)
-        widen_step_rows()
+        nc.scalar.copy(out=step_rows32[:], in_=step_rows[:])
         add_damp(4)
         add_damp(5)
-        multiply("e8", (1, 0))
+        join((0, 0), nc.vector)
+        multiply("e4", (1, 0))
         add_damp(6)
         add_damp(7)
-        quantise_h_tiles(2, 4)
-        scale8((1, 0))
-        multiply("e4", (1, 0))
+        quantise_first_half(2, HALF)
         scale4((1, 0))
-        turn_h(4)
-        turn_h(5)
+        for i in range(HALF, ROWS):
+            turn_h(i)
+        turn_step_rows()
+
+        group_e16(0, 2, nc.scalar.copy)
+        group_e16(0, 3, nc.scalar.copy)
         group_e16(0, 0, nc.vector.tensor_copy)
-        quantise_h_by_pass(4)
-        quantise_h_by_pass(5)
-        multiply("e8", (2, 0))
+        for i in range(HALF, ROWS):
+            quantise_second_half(i)
         group_e16(0, 1, nc.vector.tensor_copy)
+        multiply("e8", (2, 0))
         scale8((2, 0))
+        for g in range(PASSES):
+            quantise_e16(0, g, g + 1)
         multiply("e4", (2, 0))
         scale4((2, 0))
-        group_e16(0, 2)
-        turn_h(6)
-        turn_h(7)
-        turn_steps()
-        turn_vectors(1)
-        group_e16(0, 3)
-        quantise_h_by_pass(6)
-        quantise_h_by_pass(7)
-        multiply("e8", (3, 0))
-        scale8((3, 0))
-        multiply("e4", (3, 0))
-        quantise_e16(0)
-        scale4((3, 0))
-        for i in (3, 0, 1, 2):
-            join((i, 0), nc.gpsimd)
-        stepped((4, 0))
-        stepped((5, 0))
-        behind = [(i, j) for j in range(COLS) for i in range(ROWS)]
-        ahead = behind[6:]
+        join((2, 0), nc.gpsimd)
+        join((1, 0), nc.gpsimd)
+        for i in range(3, FIRST_ROUND_UNIT):
+            stepped_products((i, 0))
+
+        units = [(i, j) for j in range(COLS) for i in range(ROWS)]
+        rounds = units[FIRST_ROUND_UNIT:]
+        later_quarters = [(j, quarter) for j in range(1, COLS) for quarter in range(2 * PASSES)]
         done = 0
-        for s, unit in enumerate(ahead):
-            if s == 2:
-                spread_steps(1)
-                spread_steps(2)
-            stepped(unit)
-            if s in QUANT:
-                quantise_e16(QUANT[s])
-            if s in GROUP:
-                for j, quarter in GROUP[s]:
-                    group_e16(j, quarter)
-            if s == BACK:
+        for s, unit in enumerate(rounds):
+            stepped_products(unit)
+            if s in QUANTISE_ROUND:
+                quantise_e16(QUANTISE_ROUND[s], 0, PASSES)
+            if 0 <= s - FIRST_GROUPING_ROUND < len(later_quarters):
+                group_e16(*later_quarters[s - FIRST_GROUPING_ROUND], nc.scalar.copy)
+            if s == TURN_BACK_ROUND:
                 for i in range(HALF, ROWS):
                     turn_back(i)
-            want = (s + 1) * (len(behind) - TAIL) // len(ahead)
-            for late in behind[done:want]:
-                plain(late)
-            done = want
-        for late in behind[done:]:
-            plain(late)
+            due = (s + 2) * (len(units) - TAIL) // len(rounds) - 1
+            for behind in units[done:due]:
+                e16_product(behind)
+            done = due
+        for behind in units[done:]:
+            e16_product(behind)

from contextlib import ExitStack

import concourse.mybir as mybir
from concourse.masks import make_identity

K, N = 1024, 1536
FLOPS = 3 * 2 * K * K * N

F32 = mybir.dt.float32
BF16 = mybir.dt.bfloat16
I32 = mybir.dt.int32
U32 = mybir.dt.uint32
U8 = mybir.dt.uint8
FP8X4 = mybir.dt.float8_e4m3fn_x4
FP4X4 = mybir.dt.float4_e2m1fn_x4
MULT = mybir.AluOpType.mult
ADD = mybir.AluOpType.add
COPY = mybir.ActivationFunctionType.Copy

P = 128
PACK = 4
QUADRANT = 32
PASSES = K // (P * PACK)
NT = 512
COLS = N // NT
ROWS = K // P
HALF = ROWS // 2
BANKS = 8
QUARTER = NT // 2
E8_PLANE = 4

FIRST_ROUND_UNIT = 6
TAIL = 3
FIRST_GROUPING_ROUND = 1
QUANTISE_ROUND = {5: 1, 11: 2}
TURN_BACK_ROUND = 11
SUM_BUFS = 18
PART_BUFS = 6
TURNED_BACK_BUFS = HALF


def tile_damped_gram_error_s10_kernel(
    tc, gram, damp, e4_words, e4_scales, e8_words, e8_scales, e16, step4, step8, out
):
    nc = tc.nc
    step_vectors = (step8, step4)
    with ExitStack() as ctx:
        keep = ctx.enter_context(tc.tile_pool(name="keep", bufs=1))
        sums = ctx.enter_context(tc.tile_pool(name="sums", bufs=1))
        psum = ctx.enter_context(tc.psum_pool(name="psum", bufs=1))
        ctx.enter_context(tc.manual_schedule())

        free_banks = list(range(BANKS))

        def take_bank():
            b = free_banks.pop(0)
            return b, psum.tile([P, NT], F32, name="bank%d" % b, tag="bank%d" % b)

        def kept(name, shape, dtype):
            return keep.tile(shape, dtype, name=name, tag=name, align_bytes=64)

        ident = kept("ident", [P, P], F32)
        make_identity(nc, ident[:])

        planes = {}
        for j0, j1 in ((0, 1), (1, COLS)):
            for part in ("e8", "e4"):
                t = kept("%s_plane%d" % (part, j0), [P, PASSES * (j1 - j0) * NT], U8)
                for j in range(j0, j1):
                    planes[part, j] = (t, (j1 - j0) * NT, (j - j0) * NT)

        def zero_planes(j0):
            for part in ("e8", "e4"):
                nc.vector.memset(planes[part, j0][0][:].bitcast(I32), 0)

        zero_planes(0)
        step_rows = kept("step_rows", [P, P], BF16)
        nc.vector.memset(step_rows[:], 0.0)

        gram_rows = gram.rearrange("(c p e) k -> c p e k", p=P, e=2)
        out_rows = out.rearrange("(c p e) n -> c e p n", p=P, e=2)
        damp_cols = kept("damp_cols", [P, HALF, 2], BF16)
        gram_tile, e8_tile, e4_tile, e16_tile, step_words = {}, {}, {}, {}, []

        def load_gram_row(i):
            t = kept("gram%d" % i, [P, K], BF16)
            nc.sync.dma_start(out=t[:], in_=gram_rows[i // 2, :, i % 2, :])
            gram_tile[i] = (t, 0)

        def load_gram_pair(c):
            t = kept("gram%d" % (2 * c), [P, 2 * K], BF16)
            nc.sync.dma_start(out=t[:], in_=gram_rows[c].rearrange("p e k -> p (e k)"))
            gram_tile[2 * c] = (t, 0)
            gram_tile[2 * c + 1] = (t, K)

        def load_e8(j0, j1):
            t = kept("e8_codes%d" % j0, [P, PASSES, (j1 - j0) * NT], U32)
            src = e8_words.rearrange("g p n t -> p g (n t)")[:, :, PACK * NT * j0 : PACK * NT * j1]
            nc.sync.dma_start(out=t[:].bitcast(I32), in_=src.bitcast(I32))
            for j in range(j0, j1):
                e8_tile[j] = (t, (j - j0) * NT)

        def load_e4(j0, j1):
            t = kept("e4_codes%d" % j0, [P, PASSES, 2 * (j1 - j0) * NT], U8)
            src = e4_words.rearrange("g p b -> p g b")[:, :, 2 * NT * j0 : 2 * NT * j1]
            nc.sync.dma_start(out=t[:].bitcast(I32), in_=src.bitcast(I32))
            for j in range(j0, j1):
                e4_tile[j] = (t, (j - j0) * NT)

        def load_plane(part, scales, first, j0, j1):
            plane = planes[part, j0][0]
            rows = scales.bitcast(I32).rearrange("g (q r) n -> r q g n", r=4)[:, :, :, NT // 4 * j0 : NT // 4 * j1]
            for r in range(4):
                dst = plane[:].bitcast(I32)[first + r : P : QUADRANT, :]
                nc.sync.dma_start(out=dst.rearrange("q (g n) -> q g n", g=PASSES), in_=rows[r])

        def load_e16(j):
            for g in range(PASSES):
                t = kept("e16_raw%d_%d" % (g, j), [P, PACK, NT], BF16)
                src = e16.rearrange("(g p t) n -> g p t n", p=P, t=PACK)[g, :, :, NT * j : NT * (j + 1)]
                nc.sync.dma_start(out=t[:], in_=src)
                e16_tile[g, j] = t

        def load_step_words():
            for v, step in enumerate(step_vectors):
                t = kept("step_words%d" % v, [P, 1, 4], BF16)
                nc.sync.dma_start(out=t[:], in_=step.rearrange("(j p c) -> p j c", p=P, c=4)[:, 0:1, :])
                step_words.append(t)

        def load_step_rows():
            for v, step in enumerate(step_vectors):
                rows = step.rearrange("(j b p) -> j b p", b=HALF, p=P)[0]
                nc.sync.dma_start(out=step_rows[HALF * v : HALF * (v + 1), :], in_=rows)

        h_grouped = [kept("h_grouped%d" % h, [P, HALF * K], BF16) for h in range(2)]
        h_codes = [kept("h_codes%d" % h, [P, PASSES * NT], U32) for h in range(2)]
        h_plane = [kept("h_plane%d" % h, [P, PASSES * NT], U8) for h in range(2)]

        def add_damp(i):
            t, base = gram_tile[i]
            c, e = divmod(i, 2)
            diag = t[:, base + 2 * P * c + e : base + 2 * P * (c + 1) : 2]
            nc.vector.scalar_tensor_tensor(
                out=diag, in0=ident[:], scalar=damp_cols[:, c, e : e + 1], in1=diag, op0=MULT, op1=ADD
            )

        def turn_h(i):
            t, base = gram_tile[i]
            words = t[:].bitcast(F32)
            b, turned_words = take_bank()
            for g in (1, 0) if i < HALF else (0, 1):
                first = base // 2 + 2 * P * g
                for u in range(2):
                    place = slice((2 * g + u) * P, (2 * g + u + 1) * P)
                    nc.tensor.transpose(turned_words[:, place], words[:, first + u : first + 2 * P : 2], ident[:])
            dst = h_grouped[i // HALF][:].bitcast(F32).rearrange("p (i g m u) -> p i g m u", g=PASSES, i=HALF, u=2)
            src = turned_words[:].rearrange("p (g u m) -> p g m u", g=PASSES, u=2)
            nc.scalar.copy(out=dst[:, i % HALF], in_=src)
            free_banks.append(b)

        def quantise_h(h, lo, hi, source):
            nc.vector.quantize_mx(
                out=h_codes[h][:, lo:hi].bitcast(FP8X4),
                scales=h_plane[h][:, lo:hi],
                in_=h_grouped[h][:, PACK * source : PACK * (source + hi - lo)],
            )

        def quantise_first_half(i0, i1):
            quantise_h(0, i0 * PASSES * P, i1 * PASSES * P, i0 * PASSES * P)

        def quantise_second_half(i):
            for g in (1, 0):
                lo = g * NT + (i - HALF) * P
                quantise_h(1, lo, lo + P, ((i - HALF) * PASSES + g) * P)

        spread_steps = {}
        step_cols = kept("step_cols", [P, 2 * HALF], F32)

        def spread_first_steps():
            b, spread = take_bank()
            for v in range(2):
                words = step_words[v][:].rearrange("p j c -> p (j c)").bitcast(F32)
                for w in range(2):
                    place = slice((2 * v + w) * P, (2 * v + w + 1) * P)
                    nc.tensor.transpose(spread[:, place], words[:, w : w + 1].to_broadcast([P, P]), ident[:])
            both = kept("steps0", [P, 2 * NT], BF16)
            spread_steps[0] = [both[:, 0:NT], both[:, NT : 2 * NT]]
            nc.scalar.copy(
                out=both[:].bitcast(F32).rearrange("p (v n w) -> p v n w", v=2, w=2),
                in_=spread[:].rearrange("p (v w n) -> p v n w", v=2, w=2),
            )
            free_banks.append(b)

        def load_spread_steps(j):
            tiles = [kept("steps%d_%d" % (j, v), [P, NT], BF16) for v in range(2)]
            spread_steps[j] = [t[:] for t in tiles]
            for t, step in zip(tiles, step_vectors):
                nc.sync.dma_start(out=t[:], in_=step[j * NT : (j + 1) * NT].partition_broadcast(P))

        step_rows32 = kept("step_rows32", [P, P], F32)

        def turn_step_rows():
            b, turned_rows = take_bank()
            nc.tensor.transpose(turned_rows[:, 0:P], step_rows32[:], ident[:])
            nc.scalar.copy(out=step_cols[:], in_=turned_rows[:, 0 : 2 * HALF])
            free_banks.append(b)

        e16_grouped = [kept("e16_grouped%d" % j, [P, PASSES * PACK * NT], BF16) for j in range(COLS)]
        e16_codes = [kept("e16_codes%d" % j, [P, PASSES * NT], U32) for j in range(COLS)]
        e16_plane = [kept("e16_plane%d" % j, [P, PASSES * NT], U8) for j in range(COLS)]

        def group_e16(j, quarter, copy):
            g, side = divmod(quarter, 2)
            dst = e16_grouped[j][:, PACK * QUARTER * quarter : PACK * QUARTER * (quarter + 1)]
            src = e16_tile[g, j][:, :, QUARTER * side : QUARTER * (side + 1)]
            copy(
                out=dst.rearrange("p (c i t) -> p c t i", i=4, t=PACK),
                in_=src.rearrange("p t (c i) -> p c t i", i=4),
            )

        def quantise_e16(j, g0, g1):
            nc.vector.quantize_mx(
                out=e16_codes[j][:, g0 * NT : g1 * NT].bitcast(FP8X4),
                scales=e16_plane[j][:, g0 * NT : g1 * NT],
                in_=e16_grouped[j][:, PACK * g0 * NT : PACK * g1 * NT],
            )

        def error_operand(part, g, j, lo, hi):
            if part == "e16":
                cols = slice(g * NT + lo, g * NT + hi)
                return e16_codes[j][:, cols].bitcast(FP8X4), e16_plane[j][:, cols]
            plane, width, base = planes[part, j]
            cols = slice(g * width + base + lo, g * width + base + hi)
            if part == "e8":
                t, first = e8_tile[j]
                return t[:, g, first + lo : first + hi].bitcast(FP8X4), plane[E8_PLANE:P, cols]
            t, first = e4_tile[j]
            return t[:, g, 2 * (first + lo) : 2 * (first + hi)].bitcast(FP4X4), plane[:, cols]

        def h_operand(g, i0, i1):
            h = i0 // HALF
            first = (i0 * PASSES + g) * P if h == 0 else g * NT + (i0 - HALF) * P
            cols = slice(first, first + (i1 - i0) * P)
            return h_codes[h][:, cols].bitcast(FP8X4), h_plane[h][:, cols]

        product, part8, total = {}, {}, {}

        def turned(unit):
            return unit[1] == 0 and unit[0] >= HALF

        def multiply(part, unit):
            i, j = unit
            b, acc = take_bank()
            for g in (1, 0):
                if turned(unit):
                    stationary = error_operand(part, g, j, (i - HALF) * P, (i - HALF + 1) * P)
                    moving = h_operand(g, HALF, ROWS)
                else:
                    stationary = h_operand(g, i, i + 1)
                    moving = error_operand(part, g, j, 0, NT)
                nc.tensor.matmul_mx(
                    out=acc[:],
                    lhsT=stationary[0],
                    lhsT_scale=stationary[1],
                    rhs=moving[0],
                    rhs_scale=moving[1],
                    start=(g == 1),
                    stop=(g == 0),
                )
            product[part, unit] = (b, acc)

        def scale8(unit):
            i, j = unit
            b, acc = product["e8", unit]
            if turned(unit):
                step_col = step_cols[:, i - HALF : i - HALF + 1]
                nc.vector.scalar_tensor_tensor(
                    out=total[unit][:], in0=acc[:], scalar=step_col, in1=total[unit][:], op0=MULT, op1=ADD
                )
            else:
                part8[unit] = sums.tile([P, NT], F32, name="part8", tag="part8", bufs=PART_BUFS)
                nc.vector.tensor_tensor(out=part8[unit][:], in0=acc[:], in1=spread_steps[j][0], op=MULT)
            free_banks.append(b)

        def scale4(unit):
            i, j = unit
            b, acc = product["e4", unit]
            total[unit] = sums.tile([P, NT], F32, name="total", tag="total", bufs=SUM_BUFS)
            if turned(unit):
                nc.scalar.activation(out=total[unit][:], in_=acc[:], func=COPY, scale=step_cols[:, i : i + 1])
            else:
                nc.vector.tensor_tensor(out=total[unit][:], in0=acc[:], in1=spread_steps[j][1], op=MULT)
            free_banks.append(b)

        def join(unit, engine):
            engine.tensor_tensor(out=total[unit][:], in0=total[unit][:], in1=part8[unit][:], op=ADD)

        def store(unit, t):
            i, j = unit
            nc.sync.dma_start(out=out_rows[i // 2, i % 2, :, j * NT : (j + 1) * NT], in_=t[:])

        def stepped_products(unit):
            if turned(unit):
                multiply("e4", unit)
                scale4(unit)
                multiply("e8", unit)
                scale8(unit)
            else:
                multiply("e8", unit)
                scale8(unit)
                multiply("e4", unit)
                scale4(unit)
                join(unit, nc.gpsimd)

        def e16_product(unit):
            multiply("e16", unit)
            b, acc = product["e16", unit]
            nc.vector.tensor_tensor(out=total[unit][:], in0=acc[:], in1=total[unit][:], op=ADD)
            free_banks.append(b)
            if not turned(unit):
                store(unit, total[unit])

        def turn_back(i):
            b, straight = take_bank()
            for block in range(HALF):
                src = total[HALF + block, 0][:, (i - HALF) * P : (i - HALF + 1) * P]
                nc.tensor.transpose(straight[:, block * P : (block + 1) * P], src, ident[:])
            t = sums.tile([P, NT], F32, name="turned_back", tag="turned_back", bufs=TURNED_BACK_BUFS)
            nc.scalar.copy(out=t[:], in_=straight[:])
            free_banks.append(b)
            store((i, 0), t)

        nc.sync.dma_start(out=damp_cols[:], in_=damp.rearrange("(c p e) -> p c e", p=P, e=2))
        load_gram_row(0)
        load_step_words()
        load_gram_row(1)
        load_e8(0, 1)
        load_plane("e8", e8_scales, E8_PLANE, 0, 1)
        load_e4(0, 1)
        load_plane("e4", e4_scales, 0, 0, 1)
        load_gram_pair(1)
        load_step_rows()
        load_gram_pair(2)
        load_gram_pair(3)
        load_e16(0)

        add_damp(0)
        add_damp(1)
        turn_h(0)
        spread_first_steps()
        quantise_first_half(0, 1)

        zero_planes(1)
        load_plane("e8", e8_scales, E8_PLANE, 1, COLS)
        load_plane("e4", e4_scales, 0, 1, COLS)
        load_e8(1, COLS)
        load_e4(1, COLS)
        for j in range(1, COLS):
            load_spread_steps(j)
            load_e16(j)

        turn_h(1)
        quantise_first_half(1, 2)

        multiply("e8", (0, 0))
        scale8((0, 0))
        multiply("e4", (0, 0))
        add_damp(2)
        add_damp(3)
        scale4((0, 0))
        multiply("e8", (1, 0))
        scale8((1, 0))
        turn_h(2)
        turn_h(3)
        nc.scalar.copy(out=step_rows32[:], in_=step_rows[:])
        add_damp(4)
        add_damp(5)
        join((0, 0), nc.vector)
        multiply("e4", (1, 0))
        add_damp(6)
        add_damp(7)
        quantise_first_half(2, HALF)
        scale4((1, 0))
        for i in range(HALF, ROWS):
            turn_h(i)
        turn_step_rows()

        group_e16(0, 2, nc.scalar.copy)
        group_e16(0, 3, nc.scalar.copy)
        group_e16(0, 0, nc.vector.tensor_copy)
        for i in range(HALF, ROWS):
            quantise_second_half(i)
        group_e16(0, 1, nc.vector.tensor_copy)
        multiply("e8", (2, 0))
        scale8((2, 0))
        for g in range(PASSES):
            quantise_e16(0, g, g + 1)
        multiply("e4", (2, 0))
        scale4((2, 0))
        join((2, 0), nc.gpsimd)
        join((1, 0), nc.gpsimd)
        for i in range(3, FIRST_ROUND_UNIT):
            stepped_products((i, 0))

        units = [(i, j) for j in range(COLS) for i in range(ROWS)]
        rounds = units[FIRST_ROUND_UNIT:]
        later_quarters = [(j, quarter) for j in range(1, COLS) for quarter in range(2 * PASSES)]
        done = 0
        for s, unit in enumerate(rounds):
            stepped_products(unit)
            if s in QUANTISE_ROUND:
                quantise_e16(QUANTISE_ROUND[s], 0, PASSES)
            if 0 <= s - FIRST_GROUPING_ROUND < len(later_quarters):
                group_e16(*later_quarters[s - FIRST_GROUPING_ROUND], nc.scalar.copy)
            if s == TURN_BACK_ROUND:
                for i in range(HALF, ROWS):
                    turn_back(i)
            due = (s + 2) * (len(units) - TAIL) // len(rounds) - 1
            for behind in units[done:due]:
                e16_product(behind)
            done = due
        for behind in units[done:]:
            e16_product(behind)
